import numpy as np, ml_dtypes
CORES = [9,25,41,57]
N = 4
BF = ml_dtypes.bfloat16
def gentries(a):
    return np.ascontiguousarray(a.reshape(8, 16, -1).transpose(0, 2, 1)).reshape(8, -1)
def gtable(e):
    e = np.asarray(e); return np.ascontiguousarray(e.reshape(8, -1, 16).transpose(0, 2, 1)).reshape(128, -1).astype(np.int32)
V, W, SH, CH, RO = 256, 4096, 2, 2, 4
def parts(rng):
    s = rng.integers(0, 256, (N, 8, 16, W), dtype=np.uint8); x = rng.integers(0, 256, (N, 8, 16, V), dtype=np.uint8)
    r = rng.integers(0, 256, (N, 8, 16, V)); r = np.where(rng.random((N, 8, 1, V)) < 0.5, r, 64 + (r >> 1))
    nx = rng.integers(0, V, (N, 8, V)); sr = rng.integers(0, V, (N, 8, V)); ft = rng.integers(17000, 27000, (N, 8, V))
    return s, r, x, nx, sr, ft
def pack(s, r, x, nx, sr, ft):
    return {"prof": s.reshape(N, 128, W).astype(np.float32).astype(BF), "resid": np.ascontiguousarray(r.reshape(N, 128, V)).astype(np.int32), "obs": x.reshape(N, 128, V).astype(np.float32).astype(BF),
            "nx0": np.stack([gtable(a) for a in nx]), "src0": np.stack([gtable(a) for a in sr]), "fit0": np.ascontiguousarray(ft.reshape(N, 8, V)).astype(np.int32)}
def setup_inputs(rng):
    return pack(*parts(rng))
def setup_inputs_spread(rng):
    s = np.minimum(np.exp2(8 * rng.random((N, 8, 1, W))) * rng.random((N, 8, 16, W), dtype=np.float32), 255).astype(np.uint8)
    x = np.minimum(np.exp2(8 * rng.random((N, 8, 1, V))) * rng.random((N, 8, 16, V)), 255).astype(np.uint8)
    r = np.minimum(np.exp2(8 * rng.random((1, 8, 16, 1))) * rng.random((N, 8, 16, V)), 255).astype(np.int64)
    nx = np.minimum((V * rng.random((N, 8, V)) ** 3).astype(np.int64), V - 1); sr = V - 1 - np.minimum((V * rng.random((N, 8, V)) ** 3).astype(np.int64), V - 1)
    ft = np.minimum(np.exp2(16 * rng.random((N, 8, V)) ** 0.5), 65535).astype(np.int64)
    return pack(s, r, x, nx, sr, ft)
def setup_inputs_ends(rng):
    s, r, x, nx, sr, ft = parts(rng)
    s = 255 * rng.integers(0, 2, (N, 8, 16, W), dtype=np.uint8); x = 255 * rng.integers(0, 2, (N, 8, 16, V), dtype=np.uint8)
    cnt = np.clip(np.array([8, 16, 8, 0, 8, 16, 8, 8])[None, :, None] + rng.integers(-1, 2, (N, 8, V)), 0, 16)
    r = np.where(np.argsort(rng.random((N, 8, 16, V)), axis=2) < cnt[:, :, None, :], 255, 0)
    alt = 255 * (np.arange(16) & 1); r[:, 7, :, 0] = alt; r[:, 7, :, V - 1] = 255 - alt; r[N - 1, 7, 15, V - 1] = 255
    for q in range(N):
        for g in range(8):
            if (N - 1 - q + 7 - g) % 2 == 0:
                bit = rng.permutation(np.array([0, 1] + [int(b) for b in rng.integers(0, 2, 14)])).astype(np.uint8); row = (255 * bit)[:, None]
                s[q, g] = row; kind = rng.integers(0, 4, V); kind[0] = 0; kind[V - 1] = 0
                x[q, g] = np.where(kind[None, :] < 2, 255 - row, np.where(kind[None, :] == 2, row, x[q, g]))
    ft = np.where(rng.random((N, 8, V)) < 0.7, 65535, 0); ft[:, :, 0] = 65535; ft[:, :, V - 1] = 65535
    nx = np.where(rng.random((N, 8, V)) < 0.8, (V - 1) * rng.integers(0, 2, (N, 8, V)), nx); sr = np.where(rng.random((N, 8, V)) < 0.8, (V - 1) * rng.integers(0, 2, (N, 8, V)), sr)
    nx[:, :, V - 1] = V - 1; sr[:, :, V - 1] = 0
    return pack(s, r, x, nx, sr, ft)
def setup_inputs_corners(rng):
    s, r, x, nx, sr, ft = parts(rng); own = np.arange(V)
    for q in range(N):
        r[q, 0:2] = rng.integers(0, 8, (2, 16, V)) if q % 2 == 0 else rng.integers(248, 256, (2, 16, V))
    v = rng.integers(0, 2, (N, 2, 8, V)); e = 128 + np.concatenate([v, -v], axis=2)
    e = np.take_along_axis(e, np.argsort(rng.random(e.shape), axis=2), 2)
    d = np.where((own & 1) == 1, rng.choice(np.array([-129, -128, -127, -1, 0, 1, 126, 127, 128]), (N, 2, V)), 0)
    e[:, :, 0] += d >> 1; e[:, :, 15] += d - (d >> 1); r[:, 2:4] = e
    nx[:, 2:4] = 2 * rng.integers(0, V // 2, (N, 2, V)); sr[:, 2:4] = 2 * rng.integers(0, V // 2, (N, 2, V))
    top = rng.random((N, 1, V)) < 0.5; low = np.zeros((N, 16, V), np.int64)
    np.put_along_axis(low, rng.integers(0, 16, (N, 1, V)), rng.choice(np.array([0, 0, 1, 2, 100, 254, 255]), (N, 1, V)), 1)
    r[:, 4] = np.where(top, 255 - low, low)
    for q in range(N):
        for g in range(8):
            m = (q + g) % 6
            if g not in (2, 3):
                if m == 0: nx[q, g] = own; sr[q, g] = own
                if m == 1: nx[q, g] = 0; sr[q, g] = V - 1
                if m == 2: nx[q, g] = V - 1; sr[q, g] = 0
                if m == 3: nx[q, g] = own; sr[q, g] = (own + 1) % V
                if m == 4: nx[q, g] = np.stack([0 * own, 0 * own + V - 1, own])[rng.integers(0, 3, V), own]
            m = (2 * q + g) % 5
            if m == 0: ft[q, g] = 0
            if m == 1: ft[q, g] = 65535
            if m == 2: ft[q, g] = rng.choice(np.array([0, 1, 7, 8, 20000, 65279, 65280, 65281, 65535]), V)
    return pack(s, r, x, nx, sr, ft)
def setup_inputs_near(rng):
    s, r, x, nx, sr, ft = parts(rng); own = np.arange(V)
    mid = 112 + (r[:, 5:7] & 15); s = s & 3; x = x & 3; r[:, ::2] = r[:, ::2] & 3; r[:, 5:7] = mid
    sr = np.where(rng.random((N, 8, V)) < 0.25, own, sr); ft = rng.integers(285, 336, (N, 8, V))
    ft[:, 5:7] = np.where(rng.random((N, 2, V)) < 0.5, 65535, ft[:, 5:7])
    return pack(s, r, x, nx, sr, ft)
def setup_inputs_rounds(rng):
    s, r, x, nx, sr, ft = parts(rng); m = V - N; e = np.arange(m); st = (3 * e) // m
    for g in range(8):
        if g in (3, 7):
            s[:, g] = s[:, g] & 3; x[:, g] = x[:, g] & 3; r[:, g] = 112 + (r[:, g] & 7); ft[:, g] = 65535
            continue
        o = rng.permutation(V); tg = o[:N]
        for q in range(N):
            row = 255 * rng.integers(0, 2, (16, 1)); kind = rng.integers(0, 3, (1, V))
            d = np.where(kind == 0, 255, np.where(kind == 1, 255 - rng.integers(0, 101, (16, V)), rng.integers(0, 128, (16, V))))
            s[q, g] = row.astype(np.uint8); x[q, g] = np.where(row == 0, d, 255 - d).astype(np.uint8)
            mid = 112 + (r[q, g] & 7); mid[:, tg[np.arange(N) != q]] = rng.integers(0, 8, (16, N - 1)) + 248 * rng.integers(0, 2, (1, N - 1)); r[q, g] = mid
            sl = rng.permutation(o[N:]); nx[q, g, tg] = tg; sr[q, g, tg] = tg; nx[q, g, sl] = tg[(q + 1 + st) % N]
            w = 1 + (q + 3 * g) % 7; c = 8 * int(rng.integers(1, 4)) + w
            later = e % (w + 1) if (q + g) % 2 == 0 else e % 10
            off = np.where(st == 0, np.where(e < c, 1 + e % 9, -(e % 9)), np.where(st == 1, later, e % 10))
            ft[q, g] = 0; ft[q, g, sl] = np.maximum(16 * np.add.reduce(d, axis=0)[sl] + off, 0)
    return pack(s, r, x, nx, sr, ft)
def check_inputs(d):
    bad = []
    for k, lo, hi in (("prof", 0, 255), ("resid", 0, 255), ("obs", 0, 255), ("nx0", 0, V - 1), ("src0", 0, V - 1), ("fit0", 0, 65535)):
        v = np.asarray(d[k]).astype(np.float64)
        if not (np.min(v) >= lo and np.max(v) <= hi): bad.append("range of " + k)
        elif np.any(v != np.floor(v)): bad.append("whole numbers of " + k)
    return bad
def reference(prof, resid, obs, nx0, src0, fit0):
    sp = np.ascontiguousarray(prof.astype(np.float32).astype(np.int16).reshape(N, 8, 16, W).transpose(0, 1, 3, 2)).reshape(N, 8 * W, 16)
    ob = np.ascontiguousarray(obs.astype(np.float32).astype(np.int16).reshape(N, 8, 16, V).transpose(0, 1, 3, 2))
    r = resid.astype(np.int64).reshape(N, 8, 16, V); ft = fit0.astype(np.int64)
    nx = np.stack([gentries(a) for a in nx0]).astype(np.int64); sr = np.stack([gentries(a) for a in src0]).astype(np.int64)
    acc = np.zeros((N, 8), np.int64); odd = 2 * np.arange(V) + 1; first = (np.arange(8) * W)[:, None, None]; site = np.arange(16)[None, :, None]; none = 2 ** 20
    def cost(a, p):
        col = ((odd * (p + 4096)) >> SH) & (W - 1)
        return np.add.reduce(np.abs(np.take(sp[a], first + col, axis=0) - ob[a][:, None]), axis=-1, dtype=np.int64)
    for t in range(RO):
        tot = np.add.reduce(r, axis=2); r2, nx2, sr2, ft2, took = [], [], [], [], []
        for a in range(N):
            q = (a + 1 + t % (N - 1)) % N; n = nx[a]
            best = np.full((8, V), none, np.int64); bn = np.zeros((8, V), np.int64); bl = r[a]
            for z in range(CH):
                if z > 0: n = np.take_along_axis(sr[q], n, 1)
                l = np.take_along_axis(r[q], n[:, None, :], 2)
                dl = (tot[a] - np.take_along_axis(tot[q], n, 1))[:, None, :]
                p = np.add.accumulate(l, axis=1); g = cost(a, p); h = cost(a, p + dl)
                sc = np.add.accumulate(g, axis=1) - g + np.add.accumulate(h[:, ::-1], axis=1)[:, ::-1]
                sc = np.where((l + dl >= 0) & (l + dl <= 255), sc, none)
                j = np.argmin(sc, axis=1); m = np.min(sc, axis=1); better = m < best
                bl = np.where(better[:, None, :], l + np.where(site == j[:, None, :], dl, 0), bl)
                bn = np.where(better, n, bn); best = np.where(better, m, best)
            ok = best < ft[a] - (acc[a] & 7)[:, None]
            r2.append(np.where(ok[:, None, :], bl, r[a])); ft2.append(np.where(ok, best, ft[a])); sr2.append(np.where(ok, bn, sr[a]))
            nx2.append(np.where(ok, (13 * bn + best) & (V - 1), n)); took.append(np.add.reduce(ok.astype(np.int64), axis=1))
        r, nx, sr, ft = np.stack(r2), np.stack(nx2), np.stack(sr2), np.stack(ft2); acc = acc + np.stack(took)
    return {"yr": r.reshape(N, 128, V).astype(np.float32), "yf": ft.astype(np.float32), "yn": nx.astype(np.float32)}

@@ -1,0 +1,547 @@
+from concourse.mybir import AluOpType as OP, AxisListType, ActivationFunctionType as AF
+
+NC = 48
+NB = 128 - NC
+CPART = (18, 10, 10, 10)
+BIG = float(2 ** 26)
+
+SCRATCH = {
+    "S": ("sbuf", [128, 4096], "bfloat16"), "X": ("sbuf", [128, 256], "bfloat16"),
+    "XE": ("sbuf", [128, 16 * (128 + NB)], "bfloat16"),
+    "RI": ("sbuf", [128, 256], "int32"), "SI": ("sbuf", [128, 16], "int32"), "NI": ("sbuf", [128, 16], "int32"),
+    "FI": ("sbuf", [128, 256], "int32"), "FF": ("sbuf", [128, 512], "float32"),
+    "F": ("sbuf", [128, 16], "float32"), "FT": ("sbuf", [128, 16], "float32"),
+    "SN": ("sbuf", [128, 32], "bfloat16"),
+    "ip": ("sbuf", [128, 1], "int32"), "ic": ("sbuf", [128, 8], "int32"), "CF": ("sbuf", [128, 8], "float32"),
+    "dm": ("sbuf", [128, 128], "bfloat16"), "jm1": ("sbuf", [128, 128], "bfloat16"), "jb": ("sbuf", [128, 128], "bfloat16"),
+    "gm": ("sbuf", [128, 128], "bfloat16"), "gm2": ("sbuf", [128, 128], "bfloat16"), "jw": ("sbuf", [128, 256], "bfloat16"),
+    "JK": ("sbuf", [128, 384], "bfloat16"), "ODD0": ("sbuf", [128, 256], "float32"), "ODD1": ("sbuf", [128, 256], "float32"),
+    "IQ": ("sbuf", [128, 16], "float32"),
+    "SW": ("sbuf", [128, 512], "bfloat16"), "B": ("sbuf", [128, 128], "bfloat16"), "B32": ("sbuf", [128, 128], "bfloat16"),
+    "JA": ("sbuf", [128, 128], "bfloat16"), "JB": ("sbuf", [128, 128], "bfloat16"),
+    "TRI": ("sbuf", [128, 128], "bfloat16"), "HN": ("sbuf", [128, 128], "bfloat16"), "I": ("sbuf", [128, 128], "bfloat16"),
+    "IB": ("sbuf", [128, 128], "bfloat16"), "NBM": ("sbuf", [128, 128], "bfloat16"), "P22": ("sbuf", [128, 128], "bfloat16"),
+    "LG": ("sbuf", [128, 15 * 128], "bfloat16"), "LH": ("sbuf", [128, 16 * 128], "bfloat16"),
+    "ones": ("sbuf", [128, 256], "bfloat16"),
+    "KM": ("sbuf", [128, 256], "bfloat16"), "RS": ("sbuf", [128, 128], "float32"),
+    "ZS": ("sbuf", [128, 256], "bfloat16"), "XS": ("sbuf", [128, 256], "bfloat16"), "SR": ("sbuf", [128, 256], "bfloat16"),
+    "NR": ("sbuf", [128, 256], "bfloat16"),
+    "DNM": ("sbuf", [128, 32], "float32"), "SEL": ("sbuf", [128, 16], "uint16"),
+    "AI": ("sbuf", [128, 2], "int32"), "AFl": ("sbuf", [128, 2], "float32"), "AS": ("sbuf", [128, 16], "bfloat16"),
+    "AR0": ("sbuf", [128, 256], "bfloat16"), "AR1": ("sbuf", [128, 256], "bfloat16"),
+    "PN0": ("sbuf", [128, 256], "bfloat16"), "PN1": ("sbuf", [128, 256], "bfloat16"),
+    "L0": ("sbuf", [128, 256], "bfloat16"), "L1": ("sbuf", [128, 256], "bfloat16"), "N1t": ("sbuf", [128, 16], "uint16"),
+    "OC": ("sbuf", [128, 4 * NC], "uint16"), "CD": ("sbuf", [128, 64 * NC], "bfloat16"),
+    "KA0": ("psum", [128, 512], "float32"), "KA1": ("psum", [128, 512], "float32"),
+    "KB0": ("psum", [128, 512], "float32"), "KB1": ("psum", [128, 512], "float32"),
+    "PO0": ("psum", [128, 512], "float32"), "PO1": ("psum", [128, 512], "float32"),
+    "MI1": ("psum", [128, 512], "float32"), "MI2": ("psum", [128, 512], "float32"),
+}
+for _t in range(4):
+    SCRATCH["W%d" % _t] = ("sbuf", [128, 528], "bfloat16")
+    SCRATCH["ST%d" % _t] = ("sbuf", [128, 272], "bfloat16")
+for _c in range(2):
+    SCRATCH["N0t%d" % _c] = ("sbuf", [128, 16], "uint16")
+    SCRATCH["N0q%d" % _c] = ("sbuf", [128, 16], "bfloat16")
+    SCRATCH["X1%d" % _c] = ("sbuf", [128, 256], "bfloat16")
+    SCRATCH["OA%d" % _c] = ("sbuf", [128, 256], "uint16")
+    SCRATCH["OB%d" % _c] = ("sbuf", [128, 256], "uint16")
+    for _v in range(2):
+        SCRATCH["DA%d%d" % (_c, _v)] = ("sbuf", [128, 2048], "bfloat16")
+        SCRATCH["DB%d%d" % (_c, _v)] = ("sbuf", [128, 16 * NB], "bfloat16")
+        SCRATCH["I%d%d" % (_c, _v)] = ("sbuf", [128, 256], "int32")
+for _h in range(2):
+    for _n in ("K0S", "km", "XT", "Y", "OUT", "ZO", "ZR"):
+        SCRATCH[_n + str(_h)] = ("sbuf", [128, 128], "float32")
+    for _n in ("ZC", "CR", "CT", "OH", "BS", "MD"):
+        SCRATCH[_n + str(_h)] = ("sbuf", [128, 128], "bfloat16")
+    SCRATCH["TI%d" % _h] = ("sbuf", [128, 48], "int32")
+    SCRATCH["TF%d" % _h] = ("sbuf", [128, 88], "float32")
+    SCRATCH["SL%d" % _h] = ("sbuf", [128, 8], "bfloat16")
+
+NDMA = 16
+SEMAPHORES = ["sV", "sA", "sP", "sG", "sL"] + ["d%d" % k for k in range(NDMA)] + ["arr%d" % k for k in range(7)]
+PSUM = ("KA0", "KA1", "KB0", "KB1", "PO0", "PO1", "MI1", "MI2")
+
+
+def rank_program(g, core, T, topo):
+    rank = T.rank_of(core)
+    if rank is None:
+        return
+    NR_ = len(T.cores)
+    queues = {"V": g.vector, "A": g.scalar, "P": g.tensor, "G": g, "S": g.sync}
+
+    ops, last, ndma, sent = [], {}, [0], [0]
+    compn = {}
+
+    def norm(x):
+        if isinstance(x, str):
+            return (x, 0, 1 << 30)
+        return x
+
+    def op(q, fn, r=(), w=(), comp=None, amt=1):
+        me = len(ops)
+        deps = set()
+        for name, a, b in [norm(x) for x in r]:
+            ps = name in PSUM
+            for (a2, b2, o, iw) in last.get(name, []):
+                if ps:
+                    if ops[o]["q"] != q:
+                        deps.add(o)
+                elif iw and a < b2 and a2 < b:
+                    deps.add(o)
+        for name, a, b in [norm(x) for x in w]:
+            ps = name in PSUM
+            for (a2, b2, o, iw) in last.get(name, []):
+                if ps:
+                    if ops[o]["q"] != q or q != "P":
+                        deps.add(o)
+                elif a < b2 and a2 < b:
+                    deps.add(o)
+        for name, a, b in [norm(x) for x in w]:
+            ps = name in PSUM
+            last[name] = [e for e in last.get(name, []) if not (ps or (a <= e[0] and e[1] <= b))] + [(a, b, me, True)]
+        for name, a, b in [norm(x) for x in r]:
+            last.setdefault(name, []).append((a, b, me, False))
+        comp = comp or q
+        ci = compn.get(comp, 0)
+        compn[comp] = ci + 1
+        deps.discard(me)
+        ops.append({"q": q, "fn": fn, "deps": deps, "comp": comp, "ci": ci, "amt": amt, "sig": amt != 1, "need": []})
+        return me
+
+    def dma(q, out, in_, r=(), w=()):
+        k = ndma[0]
+        ndma[0] += 1
+        qq = queues[q]
+        op(q, lambda: qq.dma_start(out, in_), r, w, "d%d" % k, 16)
+
+    def V(name, r, w, *a, **k):
+        fn = {"tt": g.vector.tensor_tensor, "ts": g.vector.tensor_scalar, "cp": g.vector.tensor_copy, "tr": g.vector.transpose,
+              "scan": g.vector.tensor_tensor_scan, "set": g.vector.memset}[name]
+        op("V", lambda: fn(*a, **k), r, w)
+
+    def A(r, w, out, in_, func, **k):
+        op("A", lambda: g.scalar.activation(out, in_, func, **k), r, w)
+
+    def mm(r, w, out, lhsT, rhs, start, stop):
+        op("P", lambda: g.tensor.matmul(out, lhsT, rhs, start, stop), r, w)
+
+    def iota(w, out, pattern, base, cm, small=True):
+        if small:
+            op("G", lambda: g.iota(out, pattern, base, cm, allow_small_or_imprecise_dtypes=True), (), w)
+        else:
+            op("G", lambda: g.iota(out, pattern, base, cm), (), w)
+
+    def swap(bank, c0, name, ap, ncol, r):
+        for y in range(2):
+            for x in range(2):
+                mm(["SW"] + r, [bank], T[bank][:, c0 + y:c0 + ncol:2], T.SW[:, 128 * (2 * y + x):128 * (2 * y + x) + 128],
+                   ap(x), x == 0, x == 1)
+
+    def send(t, a, b, k, dst):
+        eng = topo.engines(core, dst)
+        rid, pid, _ = topo.addr(dst)
+        m = topo.mask(core, dst)
+        sent[0] += len(eng)
+        out, src = T["W%d" % t][:, 256 + a:256 + b], T["ST%d" % t][:, a:b]
+        op("G", lambda: g.remote_dma(out, src, T.sem["arr%d" % k], T.sem.sL, pid, rid, m), [("ST%d" % t, a, b)], (), "sL", 0)
+
+    def recv(t, a, b, k, src):
+        n = len(topo.engines(src, core))
+        op("N", None, (), [("W%d" % t, 256 + a, 256 + b)], "arr%d" % k, n)
+
+    dma("S", T.RI[:], T.resid[:], (), ["RI"])
+    dma("A", T.SI[:], T.src0[:], (), ["SI"])
+    dma("S", T.NI[:], T.nx0[:], (), ["NI"])
+    dma("A", T.X[:], T.obs[:], (), ["X"])
+    dma("S", T.S[:, 0:2048], T.prof[:, 0:2048], (), [("S", 0, 2048)])
+    dma("A", T.S[:, 2048:4096], T.prof[:, 2048:4096], (), [("S", 2048, 4096)])
+
+    iota(["ip"], T.ip[:], [[0, 1]], 0, 1, False)
+    iota(["dm"], T.dm[:], [[1, 128]], 0, -1)
+    V("set", (), ["FI"], T.FI[:], 0)
+    dma("S", T.FI[0:128:16, :], T.fit0[:], (), ["FI"])
+    iota(["gm"], T.gm[:], [[1, 8], [0, 16]], 0, 0)
+    iota(["jm1"], T.jm1[:], [[0, 8], [1, 16]], 1, 0)
+    iota(["jb"], T.jb[:], [[0, 8], [1, 16]], -20, 0)
+    iota(["jw"], T.jw[:], [[0, 16], [1, 16]], 0, 0)
+    V("ts", ["ip"], [("ic", 0, 1)], T.ic[:, 0:1], T.ip[:], 15, None, OP.bitwise_and)
+    V("ts", ["ip"], [("ic", 1, 2)], T.ic[:, 1:2], T.ip[:], 4, None, OP.arith_shift_right)
+    V("ts", ["ip"], [("ic", 2, 3)], T.ic[:, 2:3], T.ip[:], 4, 1, OP.arith_shift_right, OP.bitwise_and)
+    V("ts", ["ip"], [("ic", 3, 4)], T.ic[:, 3:4], T.ip[:], 31, None, OP.bitwise_and)
+    V("ts", ["ip"], [("ic", 4, 5)], T.ic[:, 4:5], T.ip[:], 5, None, OP.arith_shift_right)
+
+    def col(k, s, m, a):
+        V("ts", [("ic", s, s + 1)], [("CF", k, k + 1)], T.CF[:, k:k + 1], T.ic[:, s:s + 1], float(m), float(a), OP.mult, OP.add)
+
+    def C(k):
+        return T.CF[:, k:k + 1]
+    col(3, 2, 1, 0)
+    col(4, 2, -1, 1)
+    col(0, 0, 1, 1)
+    col(1, 0, 1, -20)
+    col(2, 1, 1, 0)
+    col(5, 0, 1, 0)
+    col(6, 3, 1, 0)
+    col(7, 4, 1, 0)
+    for y in range(2):
+        for x in range(2):
+            s = 2 * y + x
+            V("ts", ["dm", ("CF", 3, 5)], [("SW", 128 * s, 128 * s + 128)], T.SW[:, 128 * s:128 * s + 128], T.dm[:], float(16 * (x - y)),
+              C(3 if y else 4), OP.is_equal, OP.mult)
+    V("cp", ["SI"], [("SN", 0, 16)], T.SN[:, 0:16], T.SI[:])
+    V("cp", ["NI"], [("SN", 16, 32)], T.SN[:, 16:32], T.NI[:])
+    V("cp", ["NI"], ["N0t0"], T.N0t0[:], T.NI[:])
+    V("cp", ["RI"], [("ST0", 0, 256)], T.ST0[:, 0:256], T.RI[:])
+    swap("MI1", 0, "SN", lambda x: T.SN[:, x:16:2], 16, [("SN", 0, 16)])
+    V("cp", ["MI1"], [("ST0", 256, 272)], T.ST0[:, 256:272], T.MI1[:, 0:16])
+    send(0, 0, 272, 0, T.cores[(rank - 1) % NR_])
+    swap("MI2", 0, "SN", lambda x: T.SN[:, 16 + x:32:2], 16, [("SN", 16, 32)])
+    V("cp", ["MI2"], ["N0q0"], T.N0q0[:], T.MI2[:, 0:16])
+    iota(["ODD0"], T.ODD0[:], [[0, 2], [2, 128]], 1, 0)
+    iota(["ODD1"], T.ODD1[:], [[0, 2], [2, 128]], 257, 0)
+    iota([("JK", 0, 256)], T.JK[0:1, 0:256], [[16, 2], [0, 8], [1, 16]], 0, 0)
+    iota(["IQ"], T.IQ[:], [[32, 8], [0, 2]], -256, 0)
+    iota(["gm2"], T.gm2[:], [[1, 4], [0, 32]], 0, 0)
+    NX = 128 + NB
+    for k in range(16):
+        A(["X"], [("XEk", k, k + 1)], T.XE[:, k:16 * NX:16], T.X[:, 0:NX], AF.Copy)
+    V("set", (), ["ones"], T.ones[:], 1.0)
+    V("set", (), [("JK", 256, 384)], T.JK[0:1, 256:384], 4096.0)
+    V("set", (), ["ZS"], T.ZS[:], 0.0)
+    V("ts", ["jw"], ["KM"], T.KM[:], T.jw[:], 0.0, None, OP.is_gt)
+    V("ts", ["gm", "CF"], ["B"], T.B[:], T.gm[:], C(2), None, OP.is_equal)
+    V("tt", ["jm1", "B"], ["JA"], T.JA[:], T.jm1[:], T.B[:], OP.mult)
+    V("tt", ["jb", "B"], ["JB"], T.JB[:], T.jb[:], T.B[:], OP.mult)
+    V("ts", ["JA", "CF"], ["TRI"], T.TRI[:], T.JA[:], C(0), None, OP.is_ge)
+    V("ts", ["JB", "CF"], ["HN"], T.HN[:], T.JB[:], C(1), -1.0, OP.is_lt, OP.mult)
+    V("ts", ["JA", "CF"], ["I"], T.I[:], T.JA[:], C(0), None, OP.is_equal)
+    V("tt", ["I", "B"], ["IB"], T.IB[:], T.I[:], T.B[:], OP.subtract)
+    V("ts", ["B"], ["NBM"], T.NBM[:], T.B[:], -1.0, None, OP.mult)
+    V("ts", ["I"], ["P22"], T.P22[:], T.I[:], float(2 ** 22), None, OP.mult)
+    V("ts", ["jw"], ["RS"], T.RS[:], T.jw[:, 0:128], 0.0, BIG, OP.is_equal, OP.mult)
+
+    def consts2():
+        for k in range(16):
+            if k < 15:
+                V("ts", ["JA"], [("LG", k, k + 1)], T.LG[:, 128 * k:128 * k + 128], T.JA[:], float(k + 1), 32.0, OP.is_gt, OP.mult)
+            V("ts", ["JB"], [("LH", k, k + 1)], T.LH[:, 128 * k:128 * k + 128], T.JB[:], float(k - 20), 32.0, OP.is_le, OP.mult)
+        V("cp", ["FI"], [("FF", 0, 256)], T.FF[:, 0:256], T.FI[:])
+        V("tr", [("FF", 0, 256)], [("FF", 256, 512)], T.FF[:, 256:512], T.FF[:, 0:256])
+        V("cp", [("FF", 256, 512)], ["F"], T.F[:], T.FF[:, 256:512:16])
+        V("cp", ["F"], ["FT"], T.FT[:], T.F[:])
+        V("ts", ["IQ", "CF"], ["IQ"], T.IQ[:], T.IQ[:], C(6), None, OP.add)
+        V("ts", ["gm2", "CF"], ["B32"], T.B32[:], T.gm2[:], C(7), None, OP.is_equal)
+        V("set", (), ["AS"], T.AS[:], 0.0)
+        for h in range(2):
+            V("set", (), ["ZC%d" % h], T["ZC%d" % h][:], 0.0)
+            V("set", (), ["ZO%d" % h], T["ZO%d" % h][:], 0.0)
+
+    for t in range(4):
+        par = t & 1
+        W, Wn = T["W%d" % t], "W%d" % t
+        ST, STn = T["ST%d" % t], "ST%d" % t
+        n0t, n0q, x1 = "N0t%d" % par, "N0q%d" % par, "X1%d" % par
+        src_core = T.cores[(rank + 1 + t % (NR_ - 1)) % NR_]
+        if t == 0:
+            recv(0, 0, 272, 0, src_core)
+        else:
+            recv(t, 0, 128, 2 * t - 1, src_core)
+            recv(t, 128, 272, 2 * t, src_core)
+
+        def pos(c, h, bank):
+            Ln = "L%d" % c
+            a, b = 128 * h, 128 * h + 128
+            pb = T[bank]
+            mm([("JK", 256, 384), "ones"], [bank], pb[:, 128:256], T.JK[0:1, 256:384], T.ones[0:1, 0:128], True, False)
+            mm(["B", ("ST0", 0, 256)], [bank], pb[:, 128:256], T.B[:], T.ST0[:, a:b], False, False)
+            mm(["HN", (Ln, a, b)], [bank], pb[:, 128:256], T.HN[:], T[Ln][:, a:b], False, True)
+            mm([("JK", 256, 384), "ones"], [bank], pb[:, 0:128], T.JK[0:1, 256:384], T.ones[0:1, 0:128], True, False)
+            mm(["TRI", (Ln, a, b)], [bank], pb[:, 0:128], T.TRI[:], T[Ln][:, a:b], False, True)
+
+        def allowed(c):
+            mm(["B", ("ST0", 0, 256)], ["MI1"], T.MI1[:, 0:256], T.B[:], T.ST0[:, 0:256], True, False)
+            mm(["IB", "L%d" % c], ["MI1"], T.MI1[:, 0:256], T.IB[:], T["L%d" % c][:, 0:256], False, True)
+            A(["MI1", "cb"], ["AR%d" % c], T["AR%d" % c][:], T.MI1[:, 0:256], AF.Copy, bias=-127.5)
+            A(["AR%d" % c], ["AR%d" % c], T["AR%d" % c][:], T["AR%d" % c][:], AF.Abs)
+
+        def pen(c):
+            V("ts", ["AR%d" % c], ["PN%d" % c], T["PN%d" % c][:], T["AR%d" % c][:], 127.5, None, OP.is_gt)
+
+        def offsets(c, h, bank):
+            In = "I%d%d" % (c, h)
+            ib = T[In]
+            V("tt", [bank, "ODD%d" % h], [In], ib[:], T[bank][:, 0:256], T["ODD%d" % h][:], OP.mult)
+            V("ts", [In], [In], ib[:], ib[:], 2, 4095, OP.arith_shift_right, OP.bitwise_and)
+            o = ("OA%d" if h == 0 else "OB%d") % c
+            V("cp", [In], [o], T[o][:], ib[:])
+            if h == 1:
+                for v in range(2):
+                    V("cp", [In], [("OCv", 2 * c + v, 2 * c + v + 1)], T.OC[:, 2 * c + v:4 * NC:4], ib[:, 128 * v + NB:128 * v + 128])
+
+        def gat(c, v, s, n0=0, n1=None):
+            d = "D%s%d%d" % (s, c, v)
+            o = "O%s%d" % (s, c)
+            n1 = (128 if s == "A" else NB) if n1 is None else n1
+            xb = 0 if s == "A" else 2048
+            V("tt", ["S", "XEk", o], [(d, 16 * n0, 16 * n1)], T[d][:, 16 * n0:16 * n1], T.S[:, 0:4096].indirect(T[o][:, 128 * v + n0:128 * v + n1]),
+              T.XE[:, xb + 16 * n0:xb + 16 * n1], OP.subtract)
+
+        def absv(c, v, s, n0=0, n1=None):
+            d = "D%s%d%d" % (s, c, v)
+            n1 = (128 if s == "A" else NB) if n1 is None else n1
+            A([(d, 16 * n0, 16 * n1)], [(d, 16 * n0, 16 * n1)], T[d][:, 16 * n0:16 * n1], T[d][:, 16 * n0:16 * n1], AF.Abs)
+
+        def keystart(c, bank, a, b, sl):
+            mm([("JK", 0, 256), "ones"], [bank], T[bank][:, a:b], T.JK[0:1, 128 * c:128 * c + 128], T.ones[0:1, 0:b - a], True, False)
+            mm(["P22", "PN%d" % c], [bank], T[bank][:, a:b], T.P22[:], T["PN%d" % c][:, sl:sl + b - a], False, False)
+
+        def keys(c, v, s, bank):
+            d = "D%s%d%d" % (s, c, v)
+            n = 128 if s == "A" else NB
+            if v == 0:
+                keystart(c, bank, 0, n, 0 if s == "A" else 128)
+            for k in range(15 + v):
+                l = "LH" if v else "LG"
+                mm([(l, k, k + 1), d], [bank], T[bank][:, 0:n], T[l][:, 128 * k:128 * k + 128], T[d][:, k:16 * n:16], False, v == 1 and k == 15)
+
+        def cslots(a, b):
+            for s in range(a, b):
+                i = 256 - NC + s
+                A(["S", "OCv", "X"], [("CD", s, s + 1)], T.CD[:, 64 * s:64 * s + 64], T.S[:, 0:4096].indirect(T.OC[:, 4 * s:4 * s + 4]), AF.Abs,
+                  bias=T.X[:, i:i + 1], scale=-1.0)
+
+        def keysc(c, bank):
+            keystart(c, bank, NB, 128, 256 - NC)
+            for v in range(2):
+                l = "LH" if v else "LG"
+                for k in range(15 + v):
+                    mm([(l, k, k + 1), "CD"], [bank], T[bank][:, NB:128], T[l][:, 128 * k:128 * k + 128],
+                       T.CD[:, 16 * (2 * c + v) + k:64 * NC:64], False, v == 1 and k == 15)
+
+        def tail1(h):
+            sfx = str(h)
+            k1 = "KA1" if h == 0 else "KB1"
+            ti, tf = T["TI" + sfx], T["TF" + sfx]
+            c0, c1 = 8 * h, 8 * h + 8
+
+            def I_(k):
+                return ti[:, 8 * k:8 * k + 8]
+
+            def F_(k):
+                return tf[:, 8 * k:8 * k + 8]
+
+            def ri(k):
+                return ("TI" + sfx, k, k + 1)
+
+            def rf(k):
+                return ("TF" + sfx, k, k + 1)
+            V("tt", [k1, "K0S" + sfx], ["km" + sfx], T["km" + sfx][:], T[k1][:, 0:128], T["K0S" + sfx][:], OP.min)
+            V("tr", ["km" + sfx], ["XT" + sfx], T["XT" + sfx][:], T["km" + sfx][:])
+            V("scan", ["RS", "XT" + sfx], ["Y" + sfx], T["Y" + sfx][:], T.RS[:], T["XT" + sfx][:], BIG, OP.add, OP.min)
+            V("cp", ["Y" + sfx], [ri(0)], I_(0), T["Y" + sfx][:, 15:128:16])
+            V("ts", [ri(0)], [ri(1)], I_(1), I_(0), 5, None, OP.arith_shift_right)
+            V("ts", [ri(0)], [ri(2)], I_(2), I_(0), 16, None, OP.bitwise_and)
+            V("tt", [ri(1), ("FT", c0, c1)], [rf(0)], F_(0), I_(1), T.FT[:, c0:c1], OP.is_lt)
+            V("tt", [ri(2), ("DNM", c0, c1)], [rf(1)], F_(1), I_(2), T.DNM[:, c0:c1], OP.mult)
+            V("tt", [rf(1), ("DNM", 16 + c0, 16 + c1)], [rf(2)], F_(2), F_(1), T.DNM[:, 16 + c0:16 + c1], OP.add)
+            V("tt", [rf(2), rf(0)], [rf(3)], F_(3), F_(2), F_(0), OP.mult)
+            V("tt", [rf(3), ("IQ", c0, c1)], ["SL" + sfx], T["SL" + sfx][:], F_(3), T.IQ[:, c0:c1], OP.add)
+            swap("MI2", 0, "SL", lambda x: T["SL" + sfx][:, x:8:2], 8, ["SL" + sfx])
+            V("ts", [ri(0)], [ri(3)], I_(3), I_(0), 15, None, OP.bitwise_and)
+            V("cp", [ri(3)], ["ZC" + sfx], T["ZC" + sfx][:, 0:128:16], I_(3))
+            V("scan", ["KM", "ZC" + sfx], ["CR" + sfx], T["CR" + sfx][:], T.KM[:, 0:128], T["ZC" + sfx][:], 0.0, OP.mult, OP.add)
+            V("tr", ["CR" + sfx], ["CT" + sfx], T["CT" + sfx][:], T["CR" + sfx][:])
+            V("ts", ["CT" + sfx, "CF"], ["OH" + sfx], T["OH" + sfx][:], T["CT" + sfx][:], C(5), None, OP.is_equal)
+
+        def tail2(h):
+            sfx = str(h)
+            ti, tf = T["TI" + sfx], T["TF" + sfx]
+            c0, c1 = 8 * h, 8 * h + 8
+            a, b = 128 * h, 128 * h + 128
+
+            def I_(k):
+                return ti[:, 8 * k:8 * k + 8]
+
+            def F_(k):
+                return tf[:, 8 * k:8 * k + 8]
+
+            def ri(k):
+                return ("TI" + sfx, k, k + 1)
+
+            def rf(k):
+                return ("TF" + sfx, k, k + 1)
+            V("ts", ["MI2"], [("SEL", c0, c1)], T.SEL[:, c0:c1], T.MI2[:, 0:8], 256.0, None, OP.add)
+            mm(["B", ("ST0", 0, 256)], ["MI1"], T.MI1[:, 0:128], T.B[:], T.ST0[:, a:b], True, False)
+            V("cp", [(Wn, 0, 512), ("SEL", c0, c1)], ["BS" + sfx], T["BS" + sfx][:], W[:, 0:512].indirect(T.SEL[:, c0:c1]))
+            mm(["NBM", "BS" + sfx], ["MI1"], T.MI1[:, 0:128], T.NBM[:], T["BS" + sfx][:], False, True)
+            mm(["I", "BS" + sfx], ["MI2"], T.MI2[:, 0:128], T.I[:], T["BS" + sfx][:], True, True)
+            V("tt", [rf(1), (n0q, c0, c1)], [rf(4)], F_(4), F_(1), T[n0q][:, c0:c1], OP.add)
+            n1 = T[x1][:, 16 * c0:16 * c1:16]
+            if t < 3:
+                sn = "ST%d" % (t + 1)
+                so = ST[:, 256 + c0:256 + c1]
+                V("tt", [rf(4), (STn, 256 + c0, 256 + c1)], [rf(5)], F_(5), F_(4), so, OP.subtract)
+                V("tt", [rf(5), rf(0)], [rf(6)], F_(6), F_(5), F_(0), OP.mult)
+                V("tt", [rf(6), (STn, 256 + c0, 256 + c1)], [(sn, 256 + c0, 256 + c1)], T[sn][:, 256 + c0:256 + c1], F_(6), so, OP.add)
+            V("ts", [rf(4)], [rf(7)], F_(7), F_(4), 13.0, None, OP.mult)
+            V("tt", [rf(7), ri(1)], [ri(4)], I_(4), F_(7), I_(1), OP.add)
+            V("ts", [ri(4)], [ri(5)], I_(5), I_(4), 255, None, OP.bitwise_and)
+            V("tt", [ri(5), x1], [rf(8)], F_(8), I_(5), n1, OP.subtract)
+            V("tt", [rf(8), rf(0)], [rf(8)], F_(8), F_(8), F_(0), OP.mult)
+            m0 = "N0q%d" % (1 - par)
+            if t < 3:
+                V("tt", [rf(8), x1], [(m0, c0, c1)], T[m0][:, c0:c1], F_(8), n1, OP.add)
+            else:
+                V("tt", [rf(8), x1], [("ZO" + sfx, 1, 2)], T["ZO" + sfx][:, 1:128:16], F_(8), n1, OP.add)
+            V("tt", [ri(1), ("F", c0, c1)], [rf(9)], F_(9), I_(1), T.F[:, c0:c1], OP.subtract)
+            V("tt", [rf(9), rf(0)], [rf(10)], F_(10), F_(9), F_(0), OP.mult)
+            if t < 3:
+                V("tt", [rf(10), ("F", c0, c1)], [("F", c0, c1)], T.F[:, c0:c1], F_(10), T.F[:, c0:c1], OP.add)
+                V("tt", [rf(0), ("AS", c0, c1)], [("AS", c0, c1)], T.AS[:, c0:c1], F_(0), T.AS[:, c0:c1], OP.add)
+            else:
+                V("tt", [rf(10), ("F", c0, c1)], [("ZO" + sfx, 0, 1)], T["ZO" + sfx][:, 0:128:16], F_(10), T.F[:, c0:c1], OP.add)
+
+        def tail3(h):
+            sfx = str(h)
+            a, b = 128 * h, 128 * h + 128
+            V("tt", ["MI1", "OH" + sfx], ["MD" + sfx], T["MD" + sfx][:], T.MI1[:, 0:128], T["OH" + sfx][:], OP.mult)
+            if t < 3:
+                sn = "ST%d" % (t + 1)
+                V("tt", ["MI2", "MD" + sfx], [(sn, a, b)], T[sn][:, a:b], T.MI2[:, 0:128], T["MD" + sfx][:], OP.add)
+                dst = T.cores[(rank - 1 - (t + 1) % (NR_ - 1)) % NR_]
+                if h == 0:
+                    send(t + 1, 0, 128, 2 * t + 1, dst)
+                else:
+                    send(t + 1, 128, 272, 2 * t + 2, dst)
+                m0, mt = "N0q%d" % (1 - par), "N0t%d" % (1 - par)
+                c0, c1 = 8 * h, 8 * h + 8
+                swap("MI1", 0, m0, lambda x: T[m0][:, c0 + x:c1:2], 8, [(m0, c0, c1)])
+                V("cp", ["MI1"], [(mt, c0, c1)], T[mt][:, c0:c1], T.MI1[:, 0:8])
+            else:
+                V("tt", ["MI2", "MD" + sfx], ["OUT" + sfx], T["OUT" + sfx][:], T.MI2[:, 0:128], T["MD" + sfx][:], OP.add)
+                dma("S", T.yr[:, a:b], T["OUT" + sfx][:], ["OUT" + sfx], ())
+                V("tr", ["ZO" + sfx], ["ZR" + sfx], T["ZR" + sfx][:], T["ZO" + sfx][:])
+                dma("S", T.yf[:, a:b], T["ZR" + sfx][0:128:16, :], ["ZR" + sfx], ())
+                dma("A", T.yn[:, a:b], T["ZR" + sfx][1:128:16, :], ["ZR" + sfx], ())
+
+        PW = (Wn, 256, 512)
+        V("cp", [PW, n0t], [("L0", 0, 128)], T.L0[:, 0:128], W[:, 256:512].indirect(T[n0t][:, 0:8]))
+        A([PW, n0t], [("L0", 128, 256)], T.L0[:, 128:256], W[:, 256:512].indirect(T[n0t][:, 8:16]), AF.Copy)
+        pos(0, 0, "PO0")
+        V("cp", [(Wn, 512, 528)], ["ZS"], T.ZS[:, 0:256:16], W[:, 512:528])
+        V("scan", ["KM", "ZS"], ["XS"], T.XS[:], T.KM[:], T.ZS[:], 0.0, OP.mult, OP.add)
+        V("tr", ["XS"], ["SR"], T.SR[:], T.XS[:])
+        V("cp", ["SR", n0t], ["NR"], T.NR[:], T.SR[:, 0:256].indirect(T[n0t][:, 0:16]))
+        V("tr", ["NR"], [x1], T[x1][:], T.NR[:])
+        swap("MI2", 0, x1, lambda x: T[x1][:, 16 * x:256:32], 16, [x1])
+        pos(0, 1, "PO1")
+        offsets(0, 0, "PO0")
+        V("cp", ["MI2"], ["N1t"], T.N1t[:], T.MI2[:, 0:16])
+        A([PW, "N1t"], ["L1"], T.L1[:], W[:, 256:512].indirect(T.N1t[:, 0:16]), AF.Copy)
+        allowed(0)
+        A([(STn, 0, 256)], [(Wn, 0, 256)], W[:, 0:256], ST[:, 0:256], AF.Copy)
+        pos(1, 1, "PO0")
+        allowed(1)
+        gat(0, 0, "A")
+        if t == 0:
+            consts2()
+        offsets(0, 1, "PO1")
+        offsets(1, 1, "PO0")
+        pos(1, 0, "PO1")
+        pen(0)
+        pen(1)
+        offsets(1, 0, "PO1")
+        absv(0, 0, "A")
+        keys(0, 0, "A", "KA0")
+        q0 = 0
+        cslots(q0, q0 + CPART[0])
+        q0 += CPART[0]
+        gat(0, 1, "A")
+        absv(0, 1, "A")
+        keys(0, 1, "A", "KA0")
+        V("tt", [x1, n0q], [("DNM", 0, 16)], T.DNM[:, 0:16], T[x1][:, 0:256:16], T[n0q][:], OP.subtract)
+        V("ts", [("DNM", 0, 16)], [("DNM", 0, 16)], T.DNM[:, 0:16], T.DNM[:, 0:16], 0.0625, None, OP.mult)
+        V("tt", [n0q, "IQ"], [("DNM", 16, 32)], T.DNM[:, 16:32], T[n0q][:], T.IQ[:], OP.subtract)
+        if t > 0:
+            for b in range(8):
+                mm(["B32", "AS"], ["MI2"], T.MI2[:, 0:2], T.B32[:], T.AS[:, 2 * b:2 * b + 2], b == 0, b == 7)
+            V("cp", ["MI2"], ["AI"], T.AI[:], T.MI2[:, 0:2])
+            V("ts", ["AI"], ["AI"], T.AI[:], T.AI[:], 7, None, OP.bitwise_and)
+            V("cp", ["AI"], ["AFl"], T.AFl[:], T.AI[:])
+            for x in range(2):
+                V("ts", ["AFl", "F"], [("FT", 0, 16)], T.FT[:, x:16:2], T.F[:, x:16:2], T.AFl[:, x:x + 1], None, OP.subtract)
+        cslots(q0, q0 + CPART[1])
+        q0 += CPART[1]
+        gat(1, 0, "A")
+        absv(1, 0, "A")
+        keys(1, 0, "A", "KA1")
+        A(["KA0"], ["K0S0"], T.K0S0[:], T.KA0[:, 0:128], AF.Copy)
+        cslots(q0, q0 + CPART[2])
+        q0 += CPART[2]
+        gat(1, 1, "A")
+        absv(1, 1, "A")
+        keys(1, 1, "A", "KA1")
+        cslots(q0, NC)
+        keysc(0, "KB0")
+        gat(0, 0, "B")
+        gat(0, 1, "B")
+        absv(0, 0, "B")
+        absv(0, 1, "B")
+        tail1(0)
+        keysc(1, "KB1")
+        keys(0, 0, "B", "KB0")
+        keys(0, 1, "B", "KB0")
+        gat(1, 0, "B")
+        absv(1, 0, "B")
+        keys(1, 0, "B", "KB1")
+        nh = NB // 2
+        gat(1, 1, "B", 0, nh)
+        absv(1, 1, "B", 0, nh)
+        gat(1, 1, "B", nh, NB)
+        absv(1, 1, "B", nh, NB)
+        A(["KB0"], ["K0S1"], T.K0S1[:], T.KB0[:, 0:128], AF.Copy)
+        tail2(0)
+        keys(1, 1, "B", "KB1")
+        tail3(0)
+        tail1(1)
+        tail2(1)
+        tail3(1)
+
+    known = {}
+    for o in ops:
+        kn = known.setdefault(o["q"], {}) if o["q"] != "N" else {}
+        for d in sorted(o["deps"], reverse=True):
+            p = ops[d]
+            if kn.get(p["comp"], -1) >= p["ci"]:
+                continue
+            o["need"].append(d)
+            p["sig"] = True
+            for c, v in p["clock"].items():
+                if kn.get(c, -1) < v:
+                    kn[c] = v
+            kn[p["comp"]] = max(kn.get(p["comp"], -1), p["ci"])
+        o["clock"] = dict(kn)
+    names = {"V": "sV", "A": "sA", "P": "sP", "G": "sG"}
+    count = {}
+    for o in ops:
+        c = names.get(o["comp"], o["comp"])
+        q = queues.get(o["q"])
+        for d in o["need"]:
+            p = ops[d]
+            q.wait_ge(T.sem[names.get(p["comp"], p["comp"])], p["val"])
+        if o["q"] == "N":
+            count[c] = count.get(c, 0) + o["amt"]
+            o["val"] = count[c]
+            continue
+        ins = o["fn"]()
+        if o["comp"] == "sL":
+            continue
+        if o["sig"]:
+            count[c] = count.get(c, 0) + o["amt"]
+            o["val"] = count[c]
+            ins.then_inc(T.sem[c], o["amt"])
+    for c in count:
+        g.wait_ge(T.sem[c], count[c])
+    g.wait_ge(T.sem.sL, sent[0])

@@ -1,8 +1,9 @@
 from concourse.mybir import AluOpType as OP, AxisListType, ActivationFunctionType as AF
 
-NC = 48
+NC = 40
 NB = 128 - NC
-CPART = (18, 10, 10, 10)
+CPART = (16, 12, 12, 0)
+NL = 32
 BIG = float(2 ** 26)
 
 SCRATCH = {
@@ -22,16 +23,18 @@ SCRATCH = {
     "TRI": ("sbuf", [128, 128], "bfloat16"), "HN": ("sbuf", [128, 128], "bfloat16"), "I": ("sbuf", [128, 128], "bfloat16"),
     "IB": ("sbuf", [128, 128], "bfloat16"), "NBM": ("sbuf", [128, 128], "bfloat16"), "P22": ("sbuf", [128, 128], "bfloat16"),
     "LG": ("sbuf", [128, 15 * 128], "bfloat16"), "LH": ("sbuf", [128, 16 * 128], "bfloat16"),
-    "ones": ("sbuf", [128, 256], "bfloat16"),
+    "J16": ("sbuf", [128, 128], "bfloat16"), "ones": ("sbuf", [128, 256], "bfloat16"),
     "KM": ("sbuf", [128, 256], "bfloat16"), "RS": ("sbuf", [128, 128], "float32"),
-    "ZS": ("sbuf", [128, 256], "bfloat16"), "XS": ("sbuf", [128, 256], "bfloat16"), "SR": ("sbuf", [128, 256], "bfloat16"),
-    "NR": ("sbuf", [128, 256], "bfloat16"),
-    "DNM": ("sbuf", [128, 32], "float32"), "SEL": ("sbuf", [128, 16], "uint16"),
+    "XS": ("sbuf", [128, 256], "bfloat16"), "SR": ("sbuf", [128, 256], "bfloat16"), "NR": ("sbuf", [128, 256], "bfloat16"),
+    "DNM": ("sbuf", [128, 32], "float32"), "SEL": ("sbuf", [128, 16], "uint16"), "EX": ("sbuf", [128, 16], "uint16"),
     "AI": ("sbuf", [128, 2], "int32"), "AFl": ("sbuf", [128, 2], "float32"), "AS": ("sbuf", [128, 16], "bfloat16"),
     "AR0": ("sbuf", [128, 256], "bfloat16"), "AR1": ("sbuf", [128, 256], "bfloat16"),
     "PN0": ("sbuf", [128, 256], "bfloat16"), "PN1": ("sbuf", [128, 256], "bfloat16"),
     "L0": ("sbuf", [128, 256], "bfloat16"), "L1": ("sbuf", [128, 256], "bfloat16"), "N1t": ("sbuf", [128, 16], "uint16"),
     "OC": ("sbuf", [128, 4 * NC], "uint16"), "CD": ("sbuf", [128, 64 * NC], "bfloat16"),
+    "TI": ("sbuf", [128, 96], "int32"),
+    "TF": ("sbuf", [128, 160], "float32"),
+    "SL": ("sbuf", [128, 16], "bfloat16"),
     "KA0": ("psum", [128, 512], "float32"), "KA1": ("psum", [128, 512], "float32"),
     "KB0": ("psum", [128, 512], "float32"), "KB1": ("psum", [128, 512], "float32"),
     "PO0": ("psum", [128, 512], "float32"), "PO1": ("psum", [128, 512], "float32"),
@@ -50,17 +53,15 @@ for _c in range(2):
         SCRATCH["DA%d%d" % (_c, _v)] = ("sbuf", [128, 2048], "bfloat16")
         SCRATCH["DB%d%d" % (_c, _v)] = ("sbuf", [128, 16 * NB], "bfloat16")
         SCRATCH["I%d%d" % (_c, _v)] = ("sbuf", [128, 256], "int32")
-for _h in range(2):
-    for _n in ("K0S", "km", "XT", "Y", "OUT", "ZO", "ZR"):
-        SCRATCH[_n + str(_h)] = ("sbuf", [128, 128], "float32")
-    for _n in ("ZC", "CR", "CT", "OH", "BS", "MD"):
-        SCRATCH[_n + str(_h)] = ("sbuf", [128, 128], "bfloat16")
-    SCRATCH["TI%d" % _h] = ("sbuf", [128, 48], "int32")
-    SCRATCH["TF%d" % _h] = ("sbuf", [128, 88], "float32")
-    SCRATCH["SL%d" % _h] = ("sbuf", [128, 8], "bfloat16")
+    for _n in ("K0S", "km", "XT"):
+        SCRATCH[_n + str(_c)] = ("sbuf", [128, 128], "float32")
+for _n in ("Y", "OUT", "ZO", "ZR"):
+    SCRATCH[_n] = ("sbuf", [128, 256], "float32")
+for _n in ("ZC", "CR", "CT", "OH", "BS", "MD"):
+    SCRATCH[_n] = ("sbuf", [128, 256], "bfloat16")
 
 NDMA = 16
-SEMAPHORES = ["sV", "sA", "sP", "sG", "sL"] + ["d%d" % k for k in range(NDMA)] + ["arr%d" % k for k in range(7)]
+SEMAPHORES = ["sV", "sA", "sP", "sG", "sL"] + ["d%d" % k for k in range(NDMA)] + ["arr%d" % k for k in range(4)]
 PSUM = ("KA0", "KA1", "KB0", "KB1", "PO0", "PO1", "MI1", "MI2")
 
 
@@ -71,8 +72,7 @@ def rank_program(g, core, T, topo):
     NR_ = len(T.cores)
     queues = {"V": g.vector, "A": g.scalar, "P": g.tensor, "G": g, "S": g.sync}
 
-    ops, last, ndma, sent = [], {}, [0], [0]
-    compn = {}
+    ops, last, ndma, sent, compn = [], {}, [0], [0], {}
 
     def norm(x):
         if isinstance(x, str):
@@ -82,33 +82,31 @@ def rank_program(g, core, T, topo):
     def op(q, fn, r=(), w=(), comp=None, amt=1):
         me = len(ops)
         deps = set()
-        for name, a, b in [norm(x) for x in r]:
-            ps = name in PSUM
+        rr, ww = [norm(x) for x in r], [norm(x) for x in w]
+        for name, a, b in rr:
             for (a2, b2, o, iw) in last.get(name, []):
-                if ps:
+                if name in PSUM:
                     if ops[o]["q"] != q:
                         deps.add(o)
                 elif iw and a < b2 and a2 < b:
                     deps.add(o)
-        for name, a, b in [norm(x) for x in w]:
-            ps = name in PSUM
+        for name, a, b in ww:
             for (a2, b2, o, iw) in last.get(name, []):
-                if ps:
+                if name in PSUM:
                     if ops[o]["q"] != q or q != "P":
                         deps.add(o)
                 elif a < b2 and a2 < b:
                     deps.add(o)
-        for name, a, b in [norm(x) for x in w]:
+        for name, a, b in ww:
             ps = name in PSUM
             last[name] = [e for e in last.get(name, []) if not (ps or (a <= e[0] and e[1] <= b))] + [(a, b, me, True)]
-        for name, a, b in [norm(x) for x in r]:
+        for name, a, b in rr:
             last.setdefault(name, []).append((a, b, me, False))
         comp = comp or q
         ci = compn.get(comp, 0)
         compn[comp] = ci + 1
         deps.discard(me)
         ops.append({"q": q, "fn": fn, "deps": deps, "comp": comp, "ci": ci, "amt": amt, "sig": amt != 1, "need": []})
-        return me
 
     def dma(q, out, in_, r=(), w=()):
         k = ndma[0]
@@ -133,23 +131,20 @@ def rank_program(g, core, T, topo):
         else:
             op("G", lambda: g.iota(out, pattern, base, cm), (), w)
 
-    def swap(bank, c0, name, ap, ncol, r):
+    def swap(bank, ap, r):
         for y in range(2):
             for x in range(2):
-                mm(["SW"] + r, [bank], T[bank][:, c0 + y:c0 + ncol:2], T.SW[:, 128 * (2 * y + x):128 * (2 * y + x) + 128],
-                   ap(x), x == 0, x == 1)
+                mm(["SW"] + r, [bank], T[bank][:, y:16:2], T.SW[:, 128 * (2 * y + x):128 * (2 * y + x) + 128], ap(x), x == 0, x == 1)
 
-    def send(t, a, b, k, dst):
-        eng = topo.engines(core, dst)
+    def send(t, dst):
         rid, pid, _ = topo.addr(dst)
         m = topo.mask(core, dst)
-        sent[0] += len(eng)
-        out, src = T["W%d" % t][:, 256 + a:256 + b], T["ST%d" % t][:, a:b]
-        op("G", lambda: g.remote_dma(out, src, T.sem["arr%d" % k], T.sem.sL, pid, rid, m), [("ST%d" % t, a, b)], (), "sL", 0)
+        sent[0] += len(topo.engines(core, dst))
+        out, src = T["W%d" % t][:, 256:528], T["ST%d" % t][:]
+        op("G", lambda: g.remote_dma(out, src, T.sem["arr%d" % t], T.sem.sL, pid, rid, m), ["ST%d" % t], (), "sL", 0)
 
-    def recv(t, a, b, k, src):
-        n = len(topo.engines(src, core))
-        op("N", None, (), [("W%d" % t, 256 + a, 256 + b)], "arr%d" % k, n)
+    def recv(t, src):
+        op("N", None, (), [("W%d" % t, 256, 528)], "arr%d" % t, len(topo.engines(src, core)))
 
     dma("S", T.RI[:], T.resid[:], (), ["RI"])
     dma("A", T.SI[:], T.src0[:], (), ["SI"])
@@ -187,17 +182,17 @@ def rank_program(g, core, T, topo):
     col(7, 4, 1, 0)
     for y in range(2):
         for x in range(2):
-            s = 2 * y + x
-            V("ts", ["dm", ("CF", 3, 5)], [("SW", 128 * s, 128 * s + 128)], T.SW[:, 128 * s:128 * s + 128], T.dm[:], float(16 * (x - y)),
-              C(3 if y else 4), OP.is_equal, OP.mult)
+            s = 128 * (2 * y + x)
+            V("ts", ["dm", ("CF", 3, 5)], [("SW", s, s + 128)], T.SW[:, s:s + 128], T.dm[:], float(16 * (x - y)), C(3 if y else 4),
+              OP.is_equal, OP.mult)
     V("cp", ["SI"], [("SN", 0, 16)], T.SN[:, 0:16], T.SI[:])
     V("cp", ["NI"], [("SN", 16, 32)], T.SN[:, 16:32], T.NI[:])
     V("cp", ["NI"], ["N0t0"], T.N0t0[:], T.NI[:])
     V("cp", ["RI"], [("ST0", 0, 256)], T.ST0[:, 0:256], T.RI[:])
-    swap("MI1", 0, "SN", lambda x: T.SN[:, x:16:2], 16, [("SN", 0, 16)])
+    swap("MI1", lambda x: T.SN[:, x:16:2], [("SN", 0, 16)])
     V("cp", ["MI1"], [("ST0", 256, 272)], T.ST0[:, 256:272], T.MI1[:, 0:16])
-    send(0, 0, 272, 0, T.cores[(rank - 1) % NR_])
-    swap("MI2", 0, "SN", lambda x: T.SN[:, 16 + x:32:2], 16, [("SN", 16, 32)])
+    send(0, T.cores[(rank - 1) % NR_])
+    swap("MI2", lambda x: T.SN[:, 16 + x:32:2], [("SN", 16, 32)])
     V("cp", ["MI2"], ["N0q0"], T.N0q0[:], T.MI2[:, 0:16])
     iota(["ODD0"], T.ODD0[:], [[0, 2], [2, 128]], 1, 0)
     iota(["ODD1"], T.ODD1[:], [[0, 2], [2, 128]], 257, 0)
@@ -209,7 +204,8 @@ def rank_program(g, core, T, topo):
         A(["X"], [("XEk", k, k + 1)], T.XE[:, k:16 * NX:16], T.X[:, 0:NX], AF.Copy)
     V("set", (), ["ones"], T.ones[:], 1.0)
     V("set", (), [("JK", 256, 384)], T.JK[0:1, 256:384], 4096.0)
-    V("set", (), ["ZS"], T.ZS[:], 0.0)
+    V("set", (), ["J16"], T.J16[0:1, :], 16.0)
+    V("cp", ["jw"], ["EX"], T.EX[:], T.jw[:, 0:16])
     V("ts", ["jw"], ["KM"], T.KM[:], T.jw[:], 0.0, None, OP.is_gt)
     V("ts", ["gm", "CF"], ["B"], T.B[:], T.gm[:], C(2), None, OP.is_equal)
     V("tt", ["jm1", "B"], ["JA"], T.JA[:], T.jm1[:], T.B[:], OP.mult)
@@ -221,34 +217,33 @@ def rank_program(g, core, T, topo):
     V("ts", ["B"], ["NBM"], T.NBM[:], T.B[:], -1.0, None, OP.mult)
     V("ts", ["I"], ["P22"], T.P22[:], T.I[:], float(2 ** 22), None, OP.mult)
     V("ts", ["jw"], ["RS"], T.RS[:], T.jw[:, 0:128], 0.0, BIG, OP.is_equal, OP.mult)
+    for k in range(15):
+        V("ts", ["JA"], [("LG", k, k + 1)], T.LG[:, 128 * k:128 * k + 128], T.JA[:], float(k + 1), 32.0, OP.is_gt, OP.mult)
 
-    def consts2():
-        for k in range(16):
-            if k < 15:
-                V("ts", ["JA"], [("LG", k, k + 1)], T.LG[:, 128 * k:128 * k + 128], T.JA[:], float(k + 1), 32.0, OP.is_gt, OP.mult)
-            V("ts", ["JB"], [("LH", k, k + 1)], T.LH[:, 128 * k:128 * k + 128], T.JB[:], float(k - 20), 32.0, OP.is_le, OP.mult)
+    def lastconsts():
         V("cp", ["FI"], [("FF", 0, 256)], T.FF[:, 0:256], T.FI[:])
         V("tr", [("FF", 0, 256)], [("FF", 256, 512)], T.FF[:, 256:512], T.FF[:, 0:256])
         V("cp", [("FF", 256, 512)], ["F"], T.F[:], T.FF[:, 256:512:16])
-        V("cp", ["F"], ["FT"], T.FT[:], T.F[:])
+        V("ts", ["F"], ["FT"], T.FT[:], T.F[:], 32.0, None, OP.mult)
         V("ts", ["IQ", "CF"], ["IQ"], T.IQ[:], T.IQ[:], C(6), None, OP.add)
         V("ts", ["gm2", "CF"], ["B32"], T.B32[:], T.gm2[:], C(7), None, OP.is_equal)
         V("set", (), ["AS"], T.AS[:], 0.0)
-        for h in range(2):
-            V("set", (), ["ZC%d" % h], T["ZC%d" % h][:], 0.0)
-            V("set", (), ["ZO%d" % h], T["ZO%d" % h][:], 0.0)
+        V("set", (), ["ZC"], T.ZC[:], 0.0)
+        V("set", (), ["ZO"], T.ZO[:], 0.0)
+
+    def lhconsts():
+        for k in range(16):
+            A(["JB"], [("LH", k, k + 1)], T.LH[:, 128 * k:128 * k + 128], T.JB[:], AF.Sign, bias=float(19.5 - k))
+        A([("LH", 0, 16)], [("LH", 0, 16)], T.LH[:], T.LH[:], AF.Copy, scale=-16.0, bias=16.0)
 
     for t in range(4):
         par = t & 1
         W, Wn = T["W%d" % t], "W%d" % t
         ST, STn = T["ST%d" % t], "ST%d" % t
         n0t, n0q, x1 = "N0t%d" % par, "N0q%d" % par, "X1%d" % par
-        src_core = T.cores[(rank + 1 + t % (NR_ - 1)) % NR_]
-        if t == 0:
-            recv(0, 0, 272, 0, src_core)
-        else:
-            recv(t, 0, 128, 2 * t - 1, src_core)
-            recv(t, 128, 272, 2 * t, src_core)
+        m0, mt = "N0q%d" % (1 - par), "N0t%d" % (1 - par)
+        n1q = T[x1][:, 0:256:16]
+        recv(t, T.cores[(rank + 1 + t % (NR_ - 1)) % NR_])
 
         def pos(c, h, bank):
             Ln = "L%d" % c
@@ -263,8 +258,7 @@ def rank_program(g, core, T, topo):
         def allowed(c):
             mm(["B", ("ST0", 0, 256)], ["MI1"], T.MI1[:, 0:256], T.B[:], T.ST0[:, 0:256], True, False)
             mm(["IB", "L%d" % c], ["MI1"], T.MI1[:, 0:256], T.IB[:], T["L%d" % c][:, 0:256], False, True)
-            A(["MI1", "cb"], ["AR%d" % c], T["AR%d" % c][:], T.MI1[:, 0:256], AF.Copy, bias=-127.5)
-            A(["AR%d" % c], ["AR%d" % c], T["AR%d" % c][:], T["AR%d" % c][:], AF.Abs)
+            A(["MI1"], ["AR%d" % c], T["AR%d" % c][:], T.MI1[:, 0:256], AF.Abs, bias=-127.5)
 
         def pen(c):
             V("ts", ["AR%d" % c], ["PN%d" % c], T["PN%d" % c][:], T["AR%d" % c][:], 127.5, None, OP.is_gt)
@@ -276,7 +270,7 @@ def rank_program(g, core, T, topo):
             V("ts", [In], [In], ib[:], ib[:], 2, 4095, OP.arith_shift_right, OP.bitwise_and)
             o = ("OA%d" if h == 0 else "OB%d") % c
             V("cp", [In], [o], T[o][:], ib[:])
-            if h == 1:
+            if h == 1 and NC:
                 for v in range(2):
                     V("cp", [In], [("OCv", 2 * c + v, 2 * c + v + 1)], T.OC[:, 2 * c + v:4 * NC:4], ib[:, 128 * v + NB:128 * v + 128])
 
@@ -312,166 +306,126 @@ def rank_program(g, core, T, topo):
                 A(["S", "OCv", "X"], [("CD", s, s + 1)], T.CD[:, 64 * s:64 * s + 64], T.S[:, 0:4096].indirect(T.OC[:, 4 * s:4 * s + 4]), AF.Abs,
                   bias=T.X[:, i:i + 1], scale=-1.0)
 
-        def keysc(c, bank):
-            keystart(c, bank, NB, 128, 256 - NC)
+        def keysc():
+            o = T.KA0[:, 256:256 + 2 * NC]
+            mm([("JK", 0, 256), "ones"], ["KA0"], o, T.JK[0:1, 0:128], T.ones[0:1, 0:2 * NC], True, False)
+            mm(["J16", "ones"], ["KA0"], T.KA0[:, 257:256 + 2 * NC:2], T.J16[0:1, :], T.ones[0:1, 0:NC], False, False)
+            for c in range(2):
+                mm(["P22", "PN%d" % c], ["KA0"], T.KA0[:, 256 + c:256 + 2 * NC:2], T.P22[:], T["PN%d" % c][:, 256 - NC:256], False, False)
             for v in range(2):
                 l = "LH" if v else "LG"
                 for k in range(15 + v):
-                    mm([(l, k, k + 1), "CD"], [bank], T[bank][:, NB:128], T[l][:, 128 * k:128 * k + 128],
-                       T.CD[:, 16 * (2 * c + v) + k:64 * NC:64], False, v == 1 and k == 15)
+                    mm([(l, k, k + 1), "CD"], ["KA0"], o, T[l][:, 128 * k:128 * k + 128], T.CD[:, 16 * v + k:64 * NC:32], False, v == 1 and k == 15)
 
-        def tail1(h):
-            sfx = str(h)
+        def I_(k):
+            return T.TI[:, 16 * k:16 * k + 16]
+
+        def F_(k):
+            return T.TF[:, 16 * k:16 * k + 16]
+
+        def ri(k):
+            return ("TI", k, k + 1)
+
+        def rf(k):
+            return ("TF", k, k + 1)
+
+        def best(h):
+            x, a, b = str(h), 128 * h, 128 * h + 128
             k1 = "KA1" if h == 0 else "KB1"
-            ti, tf = T["TI" + sfx], T["TF" + sfx]
-            c0, c1 = 8 * h, 8 * h + 8
+            n = 128 if h == 0 else NB
+            V("tt", [k1, ("K0S" + x, 0, n)], [("km" + x, 0, n)], T["km" + x][:, 0:n], T[k1][:, 0:n], T["K0S" + x][:, 0:n], OP.min)
+            V("tr", ["km" + x], ["XT" + x], T["XT" + x][:], T["km" + x][:])
+            V("scan", ["RS", "XT" + x], [("Y", a, b)], T.Y[:, a:b], T.RS[:], T["XT" + x][:], BIG, OP.add, OP.min)
 
-            def I_(k):
-                return ti[:, 8 * k:8 * k + 8]
-
-            def F_(k):
-                return tf[:, 8 * k:8 * k + 8]
-
-            def ri(k):
-                return ("TI" + sfx, k, k + 1)
-
-            def rf(k):
-                return ("TF" + sfx, k, k + 1)
-            V("tt", [k1, "K0S" + sfx], ["km" + sfx], T["km" + sfx][:], T[k1][:, 0:128], T["K0S" + sfx][:], OP.min)
-            V("tr", ["km" + sfx], ["XT" + sfx], T["XT" + sfx][:], T["km" + sfx][:])
-            V("scan", ["RS", "XT" + sfx], ["Y" + sfx], T["Y" + sfx][:], T.RS[:], T["XT" + sfx][:], BIG, OP.add, OP.min)
-            V("cp", ["Y" + sfx], [ri(0)], I_(0), T["Y" + sfx][:, 15:128:16])
-            V("ts", [ri(0)], [ri(1)], I_(1), I_(0), 5, None, OP.arith_shift_right)
+        def accept():
+            V("cp", ["Y"], [ri(0)], I_(0), T.Y[:, 15:256:16])
             V("ts", [ri(0)], [ri(2)], I_(2), I_(0), 16, None, OP.bitwise_and)
-            V("tt", [ri(1), ("FT", c0, c1)], [rf(0)], F_(0), I_(1), T.FT[:, c0:c1], OP.is_lt)
-            V("tt", [ri(2), ("DNM", c0, c1)], [rf(1)], F_(1), I_(2), T.DNM[:, c0:c1], OP.mult)
-            V("tt", [rf(1), ("DNM", 16 + c0, 16 + c1)], [rf(2)], F_(2), F_(1), T.DNM[:, 16 + c0:16 + c1], OP.add)
+            V("tt", ["Y", "FT"], [rf(0)], F_(0), T.Y[:, 15:256:16], T.FT[:], OP.is_lt)
+            V("tt", [ri(2), ("DNM", 0, 16)], [rf(1)], F_(1), I_(2), T.DNM[:, 0:16], OP.mult)
+            V("tt", [rf(1), ("DNM", 16, 32)], [rf(2)], F_(2), F_(1), T.DNM[:, 16:32], OP.add)
             V("tt", [rf(2), rf(0)], [rf(3)], F_(3), F_(2), F_(0), OP.mult)
-            V("tt", [rf(3), ("IQ", c0, c1)], ["SL" + sfx], T["SL" + sfx][:], F_(3), T.IQ[:, c0:c1], OP.add)
-            swap("MI2", 0, "SL", lambda x: T["SL" + sfx][:, x:8:2], 8, ["SL" + sfx])
+            V("tt", [rf(3), "IQ"], ["SL"], T.SL[:], F_(3), T.IQ[:], OP.add)
+            swap("MI2", lambda x: T.SL[:, x:16:2], ["SL"])
             V("ts", [ri(0)], [ri(3)], I_(3), I_(0), 15, None, OP.bitwise_and)
-            V("cp", [ri(3)], ["ZC" + sfx], T["ZC" + sfx][:, 0:128:16], I_(3))
-            V("scan", ["KM", "ZC" + sfx], ["CR" + sfx], T["CR" + sfx][:], T.KM[:, 0:128], T["ZC" + sfx][:], 0.0, OP.mult, OP.add)
-            V("tr", ["CR" + sfx], ["CT" + sfx], T["CT" + sfx][:], T["CR" + sfx][:])
-            V("ts", ["CT" + sfx, "CF"], ["OH" + sfx], T["OH" + sfx][:], T["CT" + sfx][:], C(5), None, OP.is_equal)
+            V("cp", [ri(3)], ["ZC"], T.ZC[:, 0:256:16], I_(3))
+            V("scan", ["KM", "ZC"], ["CR"], T.CR[:], T.KM[:], T.ZC[:], 0.0, OP.mult, OP.add)
+            V("ts", ["MI2"], ["SEL"], T.SEL[:], T.MI2[:, 0:16], 256.0, None, OP.add)
+            mm(["B", ("ST0", 0, 256)], ["MI1"], T.MI1[:, 0:256], T.B[:], T.ST0[:, 0:256], True, False)
+            V("cp", [(Wn, 0, 512), "SEL"], ["BS"], T.BS[:], W[:, 0:512].indirect(T.SEL[:, 0:16]))
+            mm(["NBM", "BS"], ["MI1"], T.MI1[:, 0:256], T.NBM[:], T.BS[:], False, True)
+            mm(["I", "BS"], ["MI2"], T.MI2[:, 0:256], T.I[:], T.BS[:], True, True)
+            V("tr", ["CR"], ["CT"], T.CT[:], T.CR[:])
+            V("tt", [rf(1), n0q], [rf(4)], F_(4), F_(1), T[n0q][:], OP.add)
+            V("ts", ["CT", "CF"], ["OH"], T.OH[:], T.CT[:], C(5), None, OP.is_equal)
 
-        def tail2(h):
-            sfx = str(h)
-            ti, tf = T["TI" + sfx], T["TF" + sfx]
-            c0, c1 = 8 * h, 8 * h + 8
-            a, b = 128 * h, 128 * h + 128
+        def newlists(out, w):
+            V("tt", ["MI1", "OH"], ["MD"], T.MD[:], T.MI1[:, 0:256], T.OH[:], OP.mult)
+            V("tt", ["MI2", "MD"], w, out, T.MI2[:, 0:256], T.MD[:], OP.add)
 
-            def I_(k):
-                return ti[:, 8 * k:8 * k + 8]
+        def newsrc():
+            sn = "ST%d" % (t + 1)
+            so, wo = ST[:, 256:272], (STn, 256, 272)
+            V("tt", [rf(4), wo], [rf(5)], F_(5), F_(4), so, OP.subtract)
+            V("tt", [rf(5), rf(0)], [rf(6)], F_(6), F_(5), F_(0), OP.mult)
+            V("tt", [rf(6), wo], [(sn, 256, 272)], T[sn][:, 256:272], F_(6), so, OP.add)
 
-            def F_(k):
-                return tf[:, 8 * k:8 * k + 8]
-
-            def ri(k):
-                return ("TI" + sfx, k, k + 1)
-
-            def rf(k):
-                return ("TF" + sfx, k, k + 1)
-            V("ts", ["MI2"], [("SEL", c0, c1)], T.SEL[:, c0:c1], T.MI2[:, 0:8], 256.0, None, OP.add)
-            mm(["B", ("ST0", 0, 256)], ["MI1"], T.MI1[:, 0:128], T.B[:], T.ST0[:, a:b], True, False)
-            V("cp", [(Wn, 0, 512), ("SEL", c0, c1)], ["BS" + sfx], T["BS" + sfx][:], W[:, 0:512].indirect(T.SEL[:, c0:c1]))
-            mm(["NBM", "BS" + sfx], ["MI1"], T.MI1[:, 0:128], T.NBM[:], T["BS" + sfx][:], False, True)
-            mm(["I", "BS" + sfx], ["MI2"], T.MI2[:, 0:128], T.I[:], T["BS" + sfx][:], True, True)
-            V("tt", [rf(1), (n0q, c0, c1)], [rf(4)], F_(4), F_(1), T[n0q][:, c0:c1], OP.add)
-            n1 = T[x1][:, 16 * c0:16 * c1:16]
-            if t < 3:
-                sn = "ST%d" % (t + 1)
-                so = ST[:, 256 + c0:256 + c1]
-                V("tt", [rf(4), (STn, 256 + c0, 256 + c1)], [rf(5)], F_(5), F_(4), so, OP.subtract)
-                V("tt", [rf(5), rf(0)], [rf(6)], F_(6), F_(5), F_(0), OP.mult)
-                V("tt", [rf(6), (STn, 256 + c0, 256 + c1)], [(sn, 256 + c0, 256 + c1)], T[sn][:, 256 + c0:256 + c1], F_(6), so, OP.add)
+        def newnx(out, w):
+            V("ts", [ri(0)], [ri(1)], I_(1), I_(0), 5, None, OP.arith_shift_right)
             V("ts", [rf(4)], [rf(7)], F_(7), F_(4), 13.0, None, OP.mult)
             V("tt", [rf(7), ri(1)], [ri(4)], I_(4), F_(7), I_(1), OP.add)
             V("ts", [ri(4)], [ri(5)], I_(5), I_(4), 255, None, OP.bitwise_and)
-            V("tt", [ri(5), x1], [rf(8)], F_(8), I_(5), n1, OP.subtract)
-            V("tt", [rf(8), rf(0)], [rf(8)], F_(8), F_(8), F_(0), OP.mult)
-            m0 = "N0q%d" % (1 - par)
-            if t < 3:
-                V("tt", [rf(8), x1], [(m0, c0, c1)], T[m0][:, c0:c1], F_(8), n1, OP.add)
-            else:
-                V("tt", [rf(8), x1], [("ZO" + sfx, 1, 2)], T["ZO" + sfx][:, 1:128:16], F_(8), n1, OP.add)
-            V("tt", [ri(1), ("F", c0, c1)], [rf(9)], F_(9), I_(1), T.F[:, c0:c1], OP.subtract)
-            V("tt", [rf(9), rf(0)], [rf(10)], F_(10), F_(9), F_(0), OP.mult)
-            if t < 3:
-                V("tt", [rf(10), ("F", c0, c1)], [("F", c0, c1)], T.F[:, c0:c1], F_(10), T.F[:, c0:c1], OP.add)
-                V("tt", [rf(0), ("AS", c0, c1)], [("AS", c0, c1)], T.AS[:, c0:c1], F_(0), T.AS[:, c0:c1], OP.add)
-            else:
-                V("tt", [rf(10), ("F", c0, c1)], [("ZO" + sfx, 0, 1)], T["ZO" + sfx][:, 0:128:16], F_(10), T.F[:, c0:c1], OP.add)
+            V("tt", [ri(5), x1], [rf(8)], F_(8), I_(5), n1q, OP.subtract)
+            V("tt", [rf(8), rf(0)], [rf(9)], F_(9), F_(8), F_(0), OP.mult)
+            V("tt", [rf(9), x1], w, out, F_(9), n1q, OP.add)
 
-        def tail3(h):
-            sfx = str(h)
-            a, b = 128 * h, 128 * h + 128
-            V("tt", ["MI1", "OH" + sfx], ["MD" + sfx], T["MD" + sfx][:], T.MI1[:, 0:128], T["OH" + sfx][:], OP.mult)
-            if t < 3:
-                sn = "ST%d" % (t + 1)
-                V("tt", ["MI2", "MD" + sfx], [(sn, a, b)], T[sn][:, a:b], T.MI2[:, 0:128], T["MD" + sfx][:], OP.add)
-                dst = T.cores[(rank - 1 - (t + 1) % (NR_ - 1)) % NR_]
-                if h == 0:
-                    send(t + 1, 0, 128, 2 * t + 1, dst)
-                else:
-                    send(t + 1, 128, 272, 2 * t + 2, dst)
-                m0, mt = "N0q%d" % (1 - par), "N0t%d" % (1 - par)
-                c0, c1 = 8 * h, 8 * h + 8
-                swap("MI1", 0, m0, lambda x: T[m0][:, c0 + x:c1:2], 8, [(m0, c0, c1)])
-                V("cp", ["MI1"], [(mt, c0, c1)], T[mt][:, c0:c1], T.MI1[:, 0:8])
-            else:
-                V("tt", ["MI2", "MD" + sfx], ["OUT" + sfx], T["OUT" + sfx][:], T.MI2[:, 0:128], T["MD" + sfx][:], OP.add)
-                dma("S", T.yr[:, a:b], T["OUT" + sfx][:], ["OUT" + sfx], ())
-                V("tr", ["ZO" + sfx], ["ZR" + sfx], T["ZR" + sfx][:], T["ZO" + sfx][:])
-                dma("S", T.yf[:, a:b], T["ZR" + sfx][0:128:16, :], ["ZR" + sfx], ())
-                dma("A", T.yn[:, a:b], T["ZR" + sfx][1:128:16, :], ["ZR" + sfx], ())
+        def newf(out, w):
+            V("tt", [ri(1), "F"], [rf(5)], F_(5), I_(1), T.F[:], OP.subtract)
+            V("tt", [rf(5), rf(0)], [rf(6)], F_(6), F_(5), F_(0), OP.mult)
+            V("tt", [rf(6), "F"], w, out, F_(6), T.F[:], OP.add)
 
         PW = (Wn, 256, 512)
         V("cp", [PW, n0t], [("L0", 0, 128)], T.L0[:, 0:128], W[:, 256:512].indirect(T[n0t][:, 0:8]))
-        A([PW, n0t], [("L0", 128, 256)], T.L0[:, 128:256], W[:, 256:512].indirect(T[n0t][:, 8:16]), AF.Copy)
+        A([(Wn, 512, 528), "EX"], ["XS"], T.XS[:], W[:, 512:528].indirect(T.EX[:, 0:16]), AF.Copy)
         pos(0, 0, "PO0")
-        V("cp", [(Wn, 512, 528)], ["ZS"], T.ZS[:, 0:256:16], W[:, 512:528])
-        V("scan", ["KM", "ZS"], ["XS"], T.XS[:], T.KM[:], T.ZS[:], 0.0, OP.mult, OP.add)
         V("tr", ["XS"], ["SR"], T.SR[:], T.XS[:])
-        V("cp", ["SR", n0t], ["NR"], T.NR[:], T.SR[:, 0:256].indirect(T[n0t][:, 0:16]))
-        V("tr", ["NR"], [x1], T[x1][:], T.NR[:])
-        swap("MI2", 0, x1, lambda x: T[x1][:, 16 * x:256:32], 16, [x1])
-        pos(0, 1, "PO1")
+        A(["SR", n0t], ["NR"], T.NR[:], T.SR[:, 0:256].indirect(T[n0t][:, 0:16]), AF.Copy)
+        A([PW, n0t], [("L0", 128, 256)], T.L0[:, 128:256], W[:, 256:512].indirect(T[n0t][:, 8:16]), AF.Copy)
         offsets(0, 0, "PO0")
+        V("tr", ["NR"], [x1], T[x1][:], T.NR[:])
+        swap("MI2", lambda x: T[x1][:, 16 * x:256:32], [x1])
+        pos(0, 1, "PO1")
+        if t > 0:
+            for b in range(8):
+                mm(["B32", "AS"], ["MI1"], T.MI1[:, 0:2], T.B32[:], T.AS[:, 2 * b:2 * b + 2], b == 0, b == 7)
+        else:
+            lhconsts()
+        gat(0, 0, "A", 0, 64)
         V("cp", ["MI2"], ["N1t"], T.N1t[:], T.MI2[:, 0:16])
+        if t > 0:
+            V("cp", ["MI1"], ["AI"], T.AI[:], T.MI1[:, 0:2])
+        absv(0, 0, "A", 0, 64)
         A([PW, "N1t"], ["L1"], T.L1[:], W[:, 256:512].indirect(T.N1t[:, 0:16]), AF.Copy)
-        allowed(0)
-        A([(STn, 0, 256)], [(Wn, 0, 256)], W[:, 0:256], ST[:, 0:256], AF.Copy)
         pos(1, 1, "PO0")
+        allowed(0)
+        gat(0, 0, "A", 64, 128)
         allowed(1)
-        gat(0, 0, "A")
-        if t == 0:
-            consts2()
+        absv(0, 0, "A", 64, 128)
         offsets(0, 1, "PO1")
         offsets(1, 1, "PO0")
+        A([(STn, 0, 256)], [(Wn, 0, 256)], W[:, 0:256], ST[:, 0:256], AF.Copy)
         pos(1, 0, "PO1")
+        if t == 0:
+            lastconsts()
         pen(0)
-        pen(1)
-        offsets(1, 0, "PO1")
-        absv(0, 0, "A")
-        keys(0, 0, "A", "KA0")
         q0 = 0
+        keys(0, 0, "A", "KA0")
         cslots(q0, q0 + CPART[0])
         q0 += CPART[0]
         gat(0, 1, "A")
         absv(0, 1, "A")
         keys(0, 1, "A", "KA0")
-        V("tt", [x1, n0q], [("DNM", 0, 16)], T.DNM[:, 0:16], T[x1][:, 0:256:16], T[n0q][:], OP.subtract)
-        V("ts", [("DNM", 0, 16)], [("DNM", 0, 16)], T.DNM[:, 0:16], T.DNM[:, 0:16], 0.0625, None, OP.mult)
-        V("tt", [n0q, "IQ"], [("DNM", 16, 32)], T.DNM[:, 16:32], T[n0q][:], T.IQ[:], OP.subtract)
-        if t > 0:
-            for b in range(8):
-                mm(["B32", "AS"], ["MI2"], T.MI2[:, 0:2], T.B32[:], T.AS[:, 2 * b:2 * b + 2], b == 0, b == 7)
-            V("cp", ["MI2"], ["AI"], T.AI[:], T.MI2[:, 0:2])
-            V("ts", ["AI"], ["AI"], T.AI[:], T.AI[:], 7, None, OP.bitwise_and)
-            V("cp", ["AI"], ["AFl"], T.AFl[:], T.AI[:])
-            for x in range(2):
-                V("ts", ["AFl", "F"], [("FT", 0, 16)], T.FT[:, x:16:2], T.F[:, x:16:2], T.AFl[:, x:x + 1], None, OP.subtract)
+        offsets(1, 0, "PO1")
+        pen(1)
         cslots(q0, q0 + CPART[1])
         q0 += CPART[1]
         gat(1, 0, "A")
@@ -481,33 +435,55 @@ def rank_program(g, core, T, topo):
         cslots(q0, q0 + CPART[2])
         q0 += CPART[2]
         gat(1, 1, "A")
+        V("tt", [x1, n0q], [("DNM", 0, 16)], T.DNM[:, 0:16], n1q, T[n0q][:], OP.subtract)
+        V("tt", [n0q, "IQ"], [("DNM", 16, 32)], T.DNM[:, 16:32], T[n0q][:], T.IQ[:], OP.subtract)
+        if t > 0:
+            V("ts", ["AI"], ["AI"], T.AI[:], T.AI[:], 7, None, OP.bitwise_and)
+        V("ts", [("DNM", 0, 16)], [("DNM", 0, 16)], T.DNM[:, 0:16], T.DNM[:, 0:16], 0.0625, None, OP.mult)
+        if t > 0:
+            V("cp", ["AI"], ["AFl"], T.AFl[:], T.AI[:])
+            for x in range(2):
+                V("ts", ["AFl", "F"], [("FT", 0, 16)], T.FT[:, x:16:2], T.F[:, x:16:2], T.AFl[:, x:x + 1], 32.0, OP.subtract, OP.mult)
         absv(1, 1, "A")
-        keys(1, 1, "A", "KA1")
         cslots(q0, NC)
-        keysc(0, "KB0")
-        gat(0, 0, "B")
-        gat(0, 1, "B")
-        absv(0, 0, "B")
-        absv(0, 1, "B")
-        tail1(0)
-        keysc(1, "KB1")
-        keys(0, 0, "B", "KB0")
-        keys(0, 1, "B", "KB0")
+        keysc()
+        keys(1, 1, "A", "KA1")
+        for v in range(2):
+            gat(0, v, "B")
+            absv(0, v, "B")
+            keys(0, v, "B", "KB0")
         gat(1, 0, "B")
         absv(1, 0, "B")
         keys(1, 0, "B", "KB1")
-        nh = NB // 2
-        gat(1, 1, "B", 0, nh)
-        absv(1, 1, "B", 0, nh)
-        gat(1, 1, "B", nh, NB)
-        absv(1, 1, "B", nh, NB)
-        A(["KB0"], ["K0S1"], T.K0S1[:], T.KB0[:, 0:128], AF.Copy)
-        tail2(0)
+        gat(1, 1, "B", 0, NB - NL)
+        absv(1, 1, "B", 0, NB - NL)
+        gat(1, 1, "B", NB - NL, NB)
+        A(["KA0"], [("K0S1", NB, 128)], T.K0S1[:, NB:128], T.KA0[:, 256:256 + 2 * NC:2], AF.Copy)
+        absv(1, 1, "B", NB - NL, NB)
+        A(["KB0"], [("K0S1", 0, NB)], T.K0S1[:, 0:NB], T.KB0[:, 0:NB], AF.Copy)
+        V("tt", ["KA0", ("K0S1", NB, 128)], [("km1", NB, 128)], T.km1[:, NB:128], T.KA0[:, 257:256 + 2 * NC:2], T.K0S1[:, NB:128], OP.min)
         keys(1, 1, "B", "KB1")
-        tail3(0)
-        tail1(1)
-        tail2(1)
-        tail3(1)
+        best(0)
+        best(1)
+        accept()
+        if t < 3:
+            sn = "ST%d" % (t + 1)
+            newsrc()
+            newlists(T[sn][:, 0:256], [(sn, 0, 256)])
+            send(t + 1, T.cores[(rank - 1 - (t + 1) % (NR_ - 1)) % NR_])
+            newnx(T[m0][:], [m0])
+            swap("MI1", lambda x: T[m0][:, x:16:2], [m0])
+            newf(T.F[:], ["F"])
+            V("cp", ["MI1"], [mt], T[mt][:], T.MI1[:, 0:16])
+            V("tt", [rf(0), "AS"], ["AS"], T.AS[:], F_(0), T.AS[:], OP.add)
+        else:
+            newnx(T.ZO[:, 1:256:16], [("ZO", 1, 2)])
+            newf(T.ZO[:, 0:256:16], [("ZO", 0, 1)])
+            newlists(T.OUT[:], ["OUT"])
+            dma("S", T.yr[:], T.OUT[:], ["OUT"], ())
+            V("tr", ["ZO"], ["ZR"], T.ZR[:], T.ZO[:])
+            dma("A", T.yf[:], T.ZR[0:128:16, :], ["ZR"], ())
+            dma("S", T.yn[:], T.ZR[1:128:16, :], ["ZR"], ())
 
     known = {}
     for o in ops:

@@ -1,8 +1,8 @@
 from concourse.mybir import AluOpType as OP, AxisListType, ActivationFunctionType as AF
 
-NC = 40
+NC = 48
 NB = 128 - NC
-CPART = (16, 12, 12, 0)
+CFIRST = 24
 NL = 32
 BIG = float(2 ** 26)
 
@@ -16,25 +16,23 @@ SCRATCH = {
     "ip": ("sbuf", [128, 1], "int32"), "ic": ("sbuf", [128, 8], "int32"), "CF": ("sbuf", [128, 8], "float32"),
     "dm": ("sbuf", [128, 128], "bfloat16"), "jm1": ("sbuf", [128, 128], "bfloat16"), "jb": ("sbuf", [128, 128], "bfloat16"),
     "gm": ("sbuf", [128, 128], "bfloat16"), "gm2": ("sbuf", [128, 128], "bfloat16"), "jw": ("sbuf", [128, 256], "bfloat16"),
-    "JK": ("sbuf", [128, 384], "bfloat16"), "ODD0": ("sbuf", [128, 256], "float32"), "ODD1": ("sbuf", [128, 256], "float32"),
+    "JK": ("sbuf", [128, 384], "bfloat16"), "ODD0": ("sbuf", [128, 256], "float32"), "ODDB": ("sbuf", [128, 4 * NB], "float32"), "ODDC": ("sbuf", [128, 4 * NC], "float32"),
     "IQ": ("sbuf", [128, 16], "float32"),
     "SW": ("sbuf", [128, 512], "bfloat16"), "B": ("sbuf", [128, 128], "bfloat16"), "B32": ("sbuf", [128, 128], "bfloat16"),
-    "JA": ("sbuf", [128, 128], "bfloat16"), "JB": ("sbuf", [128, 128], "bfloat16"),
+    "BX": ("sbuf", [128, 128], "bfloat16"), "JA": ("sbuf", [128, 128], "bfloat16"), "JB": ("sbuf", [128, 128], "bfloat16"),
     "TRI": ("sbuf", [128, 128], "bfloat16"), "HN": ("sbuf", [128, 128], "bfloat16"), "I": ("sbuf", [128, 128], "bfloat16"),
     "IB": ("sbuf", [128, 128], "bfloat16"), "NBM": ("sbuf", [128, 128], "bfloat16"), "P22": ("sbuf", [128, 128], "bfloat16"),
     "LG": ("sbuf", [128, 15 * 128], "bfloat16"), "LH": ("sbuf", [128, 16 * 128], "bfloat16"),
     "J16": ("sbuf", [128, 128], "bfloat16"), "ones": ("sbuf", [128, 256], "bfloat16"),
     "KM": ("sbuf", [128, 256], "bfloat16"), "RS": ("sbuf", [128, 128], "float32"),
     "XS": ("sbuf", [128, 256], "bfloat16"), "SR": ("sbuf", [128, 256], "bfloat16"), "NR": ("sbuf", [128, 256], "bfloat16"),
-    "DNM": ("sbuf", [128, 32], "float32"), "SEL": ("sbuf", [128, 16], "uint16"), "EX": ("sbuf", [128, 16], "uint16"),
+    "D0": ("sbuf", [128, 80], "int32"), "D1": ("sbuf", [128, 80], "float32"), "FS": ("sbuf", [128, 80], "bfloat16"), "SEL": ("sbuf", [128, 16], "uint16"), "EX": ("sbuf", [128, 16], "uint16"),
     "AI": ("sbuf", [128, 2], "int32"), "AFl": ("sbuf", [128, 2], "float32"), "AS": ("sbuf", [128, 16], "bfloat16"),
-    "AR0": ("sbuf", [128, 256], "bfloat16"), "AR1": ("sbuf", [128, 256], "bfloat16"),
-    "PN0": ("sbuf", [128, 256], "bfloat16"), "PN1": ("sbuf", [128, 256], "bfloat16"),
+    "AR": ("sbuf", [128, 512], "bfloat16"), "PN": ("sbuf", [128, 512], "bfloat16"),
     "L0": ("sbuf", [128, 256], "bfloat16"), "L1": ("sbuf", [128, 256], "bfloat16"), "N1t": ("sbuf", [128, 16], "uint16"),
     "OC": ("sbuf", [128, 4 * NC], "uint16"), "CD": ("sbuf", [128, 64 * NC], "bfloat16"),
-    "TI": ("sbuf", [128, 96], "int32"),
-    "TF": ("sbuf", [128, 160], "float32"),
-    "SL": ("sbuf", [128, 16], "bfloat16"),
+    "TI": ("sbuf", [128, 48], "int32"), "TF": ("sbuf", [128, 112], "float32"),
+    "IBo": ("sbuf", [128, 4 * NB], "int32"), "IC": ("sbuf", [128, 4 * NC], "int32"), "OB": ("sbuf", [128, 4 * NB], "uint16"),
     "KA0": ("psum", [128, 512], "float32"), "KA1": ("psum", [128, 512], "float32"),
     "KB0": ("psum", [128, 512], "float32"), "KB1": ("psum", [128, 512], "float32"),
     "PO0": ("psum", [128, 512], "float32"), "PO1": ("psum", [128, 512], "float32"),
@@ -48,17 +46,18 @@ for _c in range(2):
     SCRATCH["N0q%d" % _c] = ("sbuf", [128, 16], "bfloat16")
     SCRATCH["X1%d" % _c] = ("sbuf", [128, 256], "bfloat16")
     SCRATCH["OA%d" % _c] = ("sbuf", [128, 256], "uint16")
-    SCRATCH["OB%d" % _c] = ("sbuf", [128, 256], "uint16")
+    SCRATCH["IA%d" % _c] = ("sbuf", [128, 256], "int32")
     for _v in range(2):
         SCRATCH["DA%d%d" % (_c, _v)] = ("sbuf", [128, 2048], "bfloat16")
         SCRATCH["DB%d%d" % (_c, _v)] = ("sbuf", [128, 16 * NB], "bfloat16")
-        SCRATCH["I%d%d" % (_c, _v)] = ("sbuf", [128, 256], "int32")
     for _n in ("K0S", "km", "XT"):
         SCRATCH[_n + str(_c)] = ("sbuf", [128, 128], "float32")
-for _n in ("Y", "OUT", "ZO", "ZR"):
+for _n in ("OUT", "ZO", "ZR"):
     SCRATCH[_n] = ("sbuf", [128, 256], "float32")
-for _n in ("ZC", "CR", "CT", "OH", "BS", "MD"):
+SCRATCH["Y"] = ("sbuf", [128, 256], "int32")
+for _n in ("CR", "CT", "OH", "BS", "MD"):
     SCRATCH[_n] = ("sbuf", [128, 256], "bfloat16")
+SCRATCH["ZC"] = ("sbuf", [128, 256], "int32")
 
 NDMA = 16
 SEMAPHORES = ["sV", "sA", "sP", "sG", "sL"] + ["d%d" % k for k in range(NDMA)] + ["arr%d" % k for k in range(4)]
@@ -195,10 +194,6 @@ def rank_program(g, core, T, topo):
     swap("MI2", lambda x: T.SN[:, 16 + x:32:2], [("SN", 16, 32)])
     V("cp", ["MI2"], ["N0q0"], T.N0q0[:], T.MI2[:, 0:16])
     iota(["ODD0"], T.ODD0[:], [[0, 2], [2, 128]], 1, 0)
-    iota(["ODD1"], T.ODD1[:], [[0, 2], [2, 128]], 257, 0)
-    iota([("JK", 0, 256)], T.JK[0:1, 0:256], [[16, 2], [0, 8], [1, 16]], 0, 0)
-    iota(["IQ"], T.IQ[:], [[32, 8], [0, 2]], -256, 0)
-    iota(["gm2"], T.gm2[:], [[1, 4], [0, 32]], 0, 0)
     NX = 128 + NB
     for k in range(16):
         A(["X"], [("XEk", k, k + 1)], T.XE[:, k:16 * NX:16], T.X[:, 0:NX], AF.Copy)
@@ -208,6 +203,7 @@ def rank_program(g, core, T, topo):
     V("cp", ["jw"], ["EX"], T.EX[:], T.jw[:, 0:16])
     V("ts", ["jw"], ["KM"], T.KM[:], T.jw[:], 0.0, None, OP.is_gt)
     V("ts", ["gm", "CF"], ["B"], T.B[:], T.gm[:], C(2), None, OP.is_equal)
+    V("ts", ["B"], ["BX"], T.BX[:], T.B[:], 32.0, None, OP.mult)
     V("tt", ["jm1", "B"], ["JA"], T.JA[:], T.jm1[:], T.B[:], OP.mult)
     V("tt", ["jb", "B"], ["JB"], T.JB[:], T.jb[:], T.B[:], OP.mult)
     V("ts", ["JA", "CF"], ["TRI"], T.TRI[:], T.JA[:], C(0), None, OP.is_ge)
@@ -217,8 +213,21 @@ def rank_program(g, core, T, topo):
     V("ts", ["B"], ["NBM"], T.NBM[:], T.B[:], -1.0, None, OP.mult)
     V("ts", ["I"], ["P22"], T.P22[:], T.I[:], float(2 ** 22), None, OP.mult)
     V("ts", ["jw"], ["RS"], T.RS[:], T.jw[:, 0:128], 0.0, BIG, OP.is_equal, OP.mult)
-    for k in range(15):
+    for k in range(4):
         V("ts", ["JA"], [("LG", k, k + 1)], T.LG[:, 128 * k:128 * k + 128], T.JA[:], float(k + 1), 32.0, OP.is_gt, OP.mult)
+
+    def step(name, k, base, m):
+        out = T[name][:, 128 * k:128 * k + 128]
+        op("G", lambda: g.affine_select(out, T.BX[:], [[0, 8], [m, 16]], OP.is_ge, 0.0, base, 0), ["BX"], [(name, k, k + 1)])
+    for k in range(4, 15):
+        step("LG", k, -k - 1, 1)
+    iota(["ODDC"], T.ODDC[:], [[2, NC], [0, 4]], 257 + 2 * NB, 0)
+    iota([("JK", 0, 256)], T.JK[0:1, 0:256], [[16, 2], [0, 8], [1, 16]], 0, 0)
+    for k in range(16):
+        step("LH", k, k, -1)
+    iota(["ODDB"], T.ODDB[:], [[0, 4], [2, NB]], 257, 0)
+    iota(["IQ"], T.IQ[:], [[32, 8], [0, 2]], -256, 0)
+    iota(["gm2"], T.gm2[:], [[1, 4], [0, 32]], 0, 0)
 
     def lastconsts():
         V("cp", ["FI"], [("FF", 0, 256)], T.FF[:, 0:256], T.FI[:])
@@ -228,13 +237,13 @@ def rank_program(g, core, T, topo):
         V("ts", ["IQ", "CF"], ["IQ"], T.IQ[:], T.IQ[:], C(6), None, OP.add)
         V("ts", ["gm2", "CF"], ["B32"], T.B32[:], T.gm2[:], C(7), None, OP.is_equal)
         V("set", (), ["AS"], T.AS[:], 0.0)
-        V("set", (), ["ZC"], T.ZC[:], 0.0)
+        V("set", (), ["ZC"], T.ZC[:], 0)
+        V("set", (), ["D0"], T.D0[:], 0)
+        for k in (1, 3):
+            V("ts", ["IQ"], [("D0", k, k + 1)], T.D0[:, k:80:5], T.IQ[:], 0.0, 1.0, OP.mult, OP.add)
+        V("ts", ["IQ"], [("D1", 3, 4)], T.D1[:, 3:80:5], T.IQ[:], -1.0, None, OP.mult)
+        V("cp", ["IQ"], [("D1", 4, 5)], T.D1[:, 4:80:5], T.IQ[:])
         V("set", (), ["ZO"], T.ZO[:], 0.0)
-
-    def lhconsts():
-        for k in range(16):
-            A(["JB"], [("LH", k, k + 1)], T.LH[:, 128 * k:128 * k + 128], T.JB[:], AF.Sign, bias=float(19.5 - k))
-        A([("LH", 0, 16)], [("LH", 0, 16)], T.LH[:], T.LH[:], AF.Copy, scale=-16.0, bias=16.0)
 
     for t in range(4):
         par = t & 1
@@ -245,42 +254,38 @@ def rank_program(g, core, T, topo):
         n1q = T[x1][:, 0:256:16]
         recv(t, T.cores[(rank + 1 + t % (NR_ - 1)) % NR_])
 
-        def pos(c, h, bank):
-            Ln = "L%d" % c
-            a, b = 128 * h, 128 * h + 128
-            pb = T[bank]
-            mm([("JK", 256, 384), "ones"], [bank], pb[:, 128:256], T.JK[0:1, 256:384], T.ones[0:1, 0:128], True, False)
-            mm(["B", ("ST0", 0, 256)], [bank], pb[:, 128:256], T.B[:], T.ST0[:, a:b], False, False)
-            mm(["HN", (Ln, a, b)], [bank], pb[:, 128:256], T.HN[:], T[Ln][:, a:b], False, True)
-            mm([("JK", 256, 384), "ones"], [bank], pb[:, 0:128], T.JK[0:1, 256:384], T.ones[0:1, 0:128], True, False)
-            mm(["TRI", (Ln, a, b)], [bank], pb[:, 0:128], T.TRI[:], T[Ln][:, a:b], False, True)
+        def pos0(v, bank, a, b, o):
+            mm([("JK", 256, 384), "ones"], [bank], o, T.JK[0:1, 256:384], T.ones[0:1, 0:b - a], True, False)
+            if v:
+                mm(["B", ("ST0", 0, 256)], [bank], o, T.B[:], T.ST0[:, a:b], False, False)
+
+        def pos1(c, v, bank, a, b, o):
+            m = "HN" if v else "TRI"
+            mm([m, ("L%d" % c, a, b)], [bank], o, T[m][:], T["L%d" % c][:, a:b], False, True)
+
+        def pos(c, v, bank, a, b, o):
+            pos0(v, bank, a, b, o)
+            pos1(c, v, bank, a, b, o)
 
         def allowed(c):
             mm(["B", ("ST0", 0, 256)], ["MI1"], T.MI1[:, 0:256], T.B[:], T.ST0[:, 0:256], True, False)
             mm(["IB", "L%d" % c], ["MI1"], T.MI1[:, 0:256], T.IB[:], T["L%d" % c][:, 0:256], False, True)
-            A(["MI1"], ["AR%d" % c], T["AR%d" % c][:], T.MI1[:, 0:256], AF.Abs, bias=-127.5)
+            A(["MI1"], [("AR", c, c + 1)], T.AR[:, 256 * c:256 * c + 256], T.MI1[:, 0:256], AF.Abs, bias=-127.5)
 
-        def pen(c):
-            V("ts", ["AR%d" % c], ["PN%d" % c], T["PN%d" % c][:], T["AR%d" % c][:], 127.5, None, OP.is_gt)
-
-        def offsets(c, h, bank):
-            In = "I%d%d" % (c, h)
-            ib = T[In]
-            V("tt", [bank, "ODD%d" % h], [In], ib[:], T[bank][:, 0:256], T["ODD%d" % h][:], OP.mult)
-            V("ts", [In], [In], ib[:], ib[:], 2, 4095, OP.arith_shift_right, OP.bitwise_and)
-            o = ("OA%d" if h == 0 else "OB%d") % c
-            V("cp", [In], [o], T[o][:], ib[:])
-            if h == 1 and NC:
-                for v in range(2):
-                    V("cp", [In], [("OCv", 2 * c + v, 2 * c + v + 1)], T.OC[:, 2 * c + v:4 * NC:4], ib[:, 128 * v + NB:128 * v + 128])
+        def offsets(bank, odd, o, a, b):
+            In = "IBo" if o == "OB" else "I" + o[1:]
+            ib = T[In][:, a:b]
+            V("tt", [bank, odd], [(In, a, b)], ib, T[bank][:, 0:b - a], T[odd][:, 0:b - a], OP.mult)
+            V("ts", [(In, a, b)], [(In, a, b)], ib, ib, 2, 4095, OP.arith_shift_right, OP.bitwise_and)
+            V("cp", [(In, a, b)], [(o, a, b)], T[o][:, a:b], ib)
 
         def gat(c, v, s, n0=0, n1=None):
             d = "D%s%d%d" % (s, c, v)
-            o = "O%s%d" % (s, c)
+            o, k = ("OA%d" % c, 128 * v) if s == "A" else ("OB", NB * (2 * c + v))
             n1 = (128 if s == "A" else NB) if n1 is None else n1
             xb = 0 if s == "A" else 2048
-            V("tt", ["S", "XEk", o], [(d, 16 * n0, 16 * n1)], T[d][:, 16 * n0:16 * n1], T.S[:, 0:4096].indirect(T[o][:, 128 * v + n0:128 * v + n1]),
-              T.XE[:, xb + 16 * n0:xb + 16 * n1], OP.subtract)
+            V("tt", ["S", "XEk", (o, k + n0, k + n1)], [(d, 16 * n0, 16 * n1)], T[d][:, 16 * n0:16 * n1],
+              T.S[:, 0:4096].indirect(T[o][:, k + n0:k + n1]), T.XE[:, xb + 16 * n0:xb + 16 * n1], OP.subtract)
 
         def absv(c, v, s, n0=0, n1=None):
             d = "D%s%d%d" % (s, c, v)
@@ -289,7 +294,7 @@ def rank_program(g, core, T, topo):
 
         def keystart(c, bank, a, b, sl):
             mm([("JK", 0, 256), "ones"], [bank], T[bank][:, a:b], T.JK[0:1, 128 * c:128 * c + 128], T.ones[0:1, 0:b - a], True, False)
-            mm(["P22", "PN%d" % c], [bank], T[bank][:, a:b], T.P22[:], T["PN%d" % c][:, sl:sl + b - a], False, False)
+            mm(["P22", "PN"], [bank], T[bank][:, a:b], T.P22[:], T.PN[:, 256 * c + sl:256 * c + sl + b - a], False, False)
 
         def keys(c, v, s, bank):
             d = "D%s%d%d" % (s, c, v)
@@ -303,19 +308,21 @@ def rank_program(g, core, T, topo):
         def cslots(a, b):
             for s in range(a, b):
                 i = 256 - NC + s
-                A(["S", "OCv", "X"], [("CD", s, s + 1)], T.CD[:, 64 * s:64 * s + 64], T.S[:, 0:4096].indirect(T.OC[:, 4 * s:4 * s + 4]), AF.Abs,
+                A(["S", "OC", "X"], [("CD", s, s + 1)], T.CD[:, 64 * s:64 * s + 64], T.S[:, 0:4096].indirect(T.OC[:, 4 * s:4 * s + 4]), AF.Abs,
                   bias=T.X[:, i:i + 1], scale=-1.0)
 
-        def keysc():
-            o = T.KA0[:, 256:256 + 2 * NC]
-            mm([("JK", 0, 256), "ones"], ["KA0"], o, T.JK[0:1, 0:128], T.ones[0:1, 0:2 * NC], True, False)
-            mm(["J16", "ones"], ["KA0"], T.KA0[:, 257:256 + 2 * NC:2], T.J16[0:1, :], T.ones[0:1, 0:NC], False, False)
+        def keysc(s0, s1):
+            n, o = s1 - s0, T.KB0[:, 256 + 2 * s0:256 + 2 * s1]
+            mm([("JK", 0, 256), "ones"], ["KB0"], o, T.JK[0:1, 0:128], T.ones[0:1, 0:2 * n], True, False)
+            mm(["J16", "ones"], ["KB0"], T.KB0[:, 257 + 2 * s0:256 + 2 * s1:2], T.J16[0:1, :], T.ones[0:1, 0:n], False, False)
             for c in range(2):
-                mm(["P22", "PN%d" % c], ["KA0"], T.KA0[:, 256 + c:256 + 2 * NC:2], T.P22[:], T["PN%d" % c][:, 256 - NC:256], False, False)
+                i = 256 * c + 256 - NC
+                mm(["P22", "PN"], ["KB0"], T.KB0[:, 256 + 2 * s0 + c:256 + 2 * s1:2], T.P22[:], T.PN[:, i + s0:i + s1], False, False)
             for v in range(2):
                 l = "LH" if v else "LG"
                 for k in range(15 + v):
-                    mm([(l, k, k + 1), "CD"], ["KA0"], o, T[l][:, 128 * k:128 * k + 128], T.CD[:, 16 * v + k:64 * NC:32], False, v == 1 and k == 15)
+                    mm([(l, k, k + 1), ("CD", s0, s1)], ["KB0"], o, T[l][:, 128 * k:128 * k + 128],
+                       T.CD[:, 64 * s0 + 16 * v + k:64 * s1:32], False, v == 1 and k == 15)
 
         def I_(k):
             return T.TI[:, 16 * k:16 * k + 16]
@@ -328,6 +335,11 @@ def rank_program(g, core, T, topo):
 
         def rf(k):
             return ("TF", k, k + 1)
+        key, acc, nsel = T.Y[:, 15:256:16], T.D0[:, 4:80:5], T.FS[:, 2:80:5]
+
+        def n0steps(n, r):
+            V("ts", r, [("D1", 1, 2)], T.D1[:, 1:80:5], n, -1.0, None, OP.mult)
+            V("cp", r, [("D1", 2, 3)], T.D1[:, 2:80:5], n)
 
         def best(h):
             x, a, b = str(h), 128 * h, 128 * h + 128
@@ -337,26 +349,27 @@ def rank_program(g, core, T, topo):
             V("tr", ["km" + x], ["XT" + x], T["XT" + x][:], T["km" + x][:])
             V("scan", ["RS", "XT" + x], [("Y", a, b)], T.Y[:, a:b], T.RS[:], T["XT" + x][:], BIG, OP.add, OP.min)
 
+        def site(h, part):
+            a, b = 128 * h, 128 * h + 128
+            if part == 0:
+                V("ts", [("Y", a, b)], [("ZC", a, b)], T.ZC[:, a:b:16], T.Y[:, a + 15:b:16], 15, None, OP.bitwise_and)
+                V("scan", ["KM", ("ZC", a, b)], [("CR", a, b)], T.CR[:, a:b], T.KM[:, a:b], T.ZC[:, a:b], 0.0, OP.mult, OP.add)
+                V("tr", [("CR", a, b)], [("CT", a, b)], T.CT[:, a:b], T.CR[:, a:b])
+            else:
+                V("ts", [("CT", a, b), "CF"], [("OH", a, b)], T.OH[:, a:b], T.CT[:, a:b], C(5), None, OP.is_equal)
+
         def accept():
-            V("cp", ["Y"], [ri(0)], I_(0), T.Y[:, 15:256:16])
-            V("ts", [ri(0)], [ri(2)], I_(2), I_(0), 16, None, OP.bitwise_and)
-            V("tt", ["Y", "FT"], [rf(0)], F_(0), T.Y[:, 15:256:16], T.FT[:], OP.is_lt)
-            V("tt", [ri(2), ("DNM", 0, 16)], [rf(1)], F_(1), I_(2), T.DNM[:, 0:16], OP.mult)
-            V("tt", [rf(1), ("DNM", 16, 32)], [rf(2)], F_(2), F_(1), T.DNM[:, 16:32], OP.add)
-            V("tt", [rf(2), rf(0)], [rf(3)], F_(3), F_(2), F_(0), OP.mult)
-            V("tt", [rf(3), "IQ"], ["SL"], T.SL[:], F_(3), T.IQ[:], OP.add)
-            swap("MI2", lambda x: T.SL[:, x:16:2], ["SL"])
-            V("ts", [ri(0)], [ri(3)], I_(3), I_(0), 15, None, OP.bitwise_and)
-            V("cp", [ri(3)], ["ZC"], T.ZC[:, 0:256:16], I_(3))
-            V("scan", ["KM", "ZC"], ["CR"], T.CR[:], T.KM[:], T.ZC[:], 0.0, OP.mult, OP.add)
+            V("ts", ["Y"], [("D0", 2, 3)], T.D0[:, 2:80:5], key, 4, 1, OP.arith_shift_right, OP.bitwise_and)
+            V("tt", ["Y", "FT"], [("D0", 4, 5)], acc, key, T.FT[:], OP.is_lt)
+            V("scan", ["D0", "D1"], ["FS"], T.FS[:], T.D0[:], T.D1[:], 0.0, OP.mult, OP.add)
+            swap("MI2", lambda x: T.FS[:, 4 + 5 * x:80:10], ["FS"])
+            site(1, 0)
             V("ts", ["MI2"], ["SEL"], T.SEL[:], T.MI2[:, 0:16], 256.0, None, OP.add)
             mm(["B", ("ST0", 0, 256)], ["MI1"], T.MI1[:, 0:256], T.B[:], T.ST0[:, 0:256], True, False)
             V("cp", [(Wn, 0, 512), "SEL"], ["BS"], T.BS[:], W[:, 0:512].indirect(T.SEL[:, 0:16]))
             mm(["NBM", "BS"], ["MI1"], T.MI1[:, 0:256], T.NBM[:], T.BS[:], False, True)
             mm(["I", "BS"], ["MI2"], T.MI2[:, 0:256], T.I[:], T.BS[:], True, True)
-            V("tr", ["CR"], ["CT"], T.CT[:], T.CR[:])
-            V("tt", [rf(1), n0q], [rf(4)], F_(4), F_(1), T[n0q][:], OP.add)
-            V("ts", ["CT", "CF"], ["OH"], T.OH[:], T.CT[:], C(5), None, OP.is_equal)
+            site(1, 1)
 
         def newlists(out, w):
             V("tt", ["MI1", "OH"], ["MD"], T.MD[:], T.MI1[:, 0:256], T.OH[:], OP.mult)
@@ -365,88 +378,76 @@ def rank_program(g, core, T, topo):
         def newsrc():
             sn = "ST%d" % (t + 1)
             so, wo = ST[:, 256:272], (STn, 256, 272)
-            V("tt", [rf(4), wo], [rf(5)], F_(5), F_(4), so, OP.subtract)
-            V("tt", [rf(5), rf(0)], [rf(6)], F_(6), F_(5), F_(0), OP.mult)
-            V("tt", [rf(6), wo], [(sn, 256, 272)], T[sn][:, 256:272], F_(6), so, OP.add)
+            V("tt", ["FS", wo], [rf(0)], F_(0), nsel, so, OP.subtract)
+            V("tt", [rf(0), ("D0", 4, 5)], [rf(1)], F_(1), F_(0), acc, OP.mult)
+            V("tt", [rf(1), wo], [(sn, 256, 272)], T[sn][:, 256:272], F_(1), so, OP.add)
 
         def newnx(out, w):
-            V("ts", [ri(0)], [ri(1)], I_(1), I_(0), 5, None, OP.arith_shift_right)
-            V("ts", [rf(4)], [rf(7)], F_(7), F_(4), 13.0, None, OP.mult)
-            V("tt", [rf(7), ri(1)], [ri(4)], I_(4), F_(7), I_(1), OP.add)
-            V("ts", [ri(4)], [ri(5)], I_(5), I_(4), 255, None, OP.bitwise_and)
-            V("tt", [ri(5), x1], [rf(8)], F_(8), I_(5), n1q, OP.subtract)
-            V("tt", [rf(8), rf(0)], [rf(9)], F_(9), F_(8), F_(0), OP.mult)
-            V("tt", [rf(9), x1], w, out, F_(9), n1q, OP.add)
+            V("ts", ["FS"], [rf(2)], F_(2), nsel, 416.0, None, OP.mult)
+            V("tt", [rf(2), "Y"], [ri(0)], I_(0), F_(2), key, OP.add)
+            V("ts", [ri(0)], [ri(1)], I_(1), I_(0), 5, 255, OP.arith_shift_right, OP.bitwise_and)
+            V("tt", [ri(1), x1], [rf(3)], F_(3), I_(1), n1q, OP.subtract)
+            V("tt", [rf(3), ("D0", 4, 5)], [rf(4)], F_(4), F_(3), acc, OP.mult)
+            V("tt", [rf(4), x1], w, out, F_(4), n1q, OP.add)
 
         def newf(out, w):
-            V("tt", [ri(1), "F"], [rf(5)], F_(5), I_(1), T.F[:], OP.subtract)
-            V("tt", [rf(5), rf(0)], [rf(6)], F_(6), F_(5), F_(0), OP.mult)
+            V("ts", ["Y"], [ri(2)], I_(2), key, 5, None, OP.arith_shift_right)
+            V("tt", [ri(2), "F"], [rf(5)], F_(5), I_(2), T.F[:], OP.subtract)
+            V("tt", [rf(5), ("D0", 4, 5)], [rf(6)], F_(6), F_(5), acc, OP.mult)
             V("tt", [rf(6), "F"], w, out, F_(6), T.F[:], OP.add)
 
         PW = (Wn, 256, 512)
         V("cp", [PW, n0t], [("L0", 0, 128)], T.L0[:, 0:128], W[:, 256:512].indirect(T[n0t][:, 0:8]))
         A([(Wn, 512, 528), "EX"], ["XS"], T.XS[:], W[:, 512:528].indirect(T.EX[:, 0:16]), AF.Copy)
-        pos(0, 0, "PO0")
+        oA = T.PO0[:, 0:128]
+        pos0(0, "PO0", 0, 128, oA)
+        pos0(1, "PO1", 0, 128, T.PO1[:, 0:128])
+        pos1(0, 0, "PO0", 0, 128, oA)
+        pos1(0, 1, "PO1", 0, 128, T.PO1[:, 0:128])
         V("tr", ["XS"], ["SR"], T.SR[:], T.XS[:])
         A(["SR", n0t], ["NR"], T.NR[:], T.SR[:, 0:256].indirect(T[n0t][:, 0:16]), AF.Copy)
         A([PW, n0t], [("L0", 128, 256)], T.L0[:, 128:256], W[:, 256:512].indirect(T[n0t][:, 8:16]), AF.Copy)
-        offsets(0, 0, "PO0")
+        offsets("PO0", "ODD0", "OA0", 0, 128)
         V("tr", ["NR"], [x1], T[x1][:], T.NR[:])
-        swap("MI2", lambda x: T[x1][:, 16 * x:256:32], [x1])
-        pos(0, 1, "PO1")
-        if t > 0:
-            for b in range(8):
-                mm(["B32", "AS"], ["MI1"], T.MI1[:, 0:2], T.B32[:], T.AS[:, 2 * b:2 * b + 2], b == 0, b == 7)
-        else:
-            lhconsts()
         gat(0, 0, "A", 0, 64)
+        swap("MI2", lambda x: T[x1][:, 16 * x:256:32], [x1])
+        if t == 0:
+            A([(STn, 0, 256)], [(Wn, 0, 256)], W[:, 0:256], ST[:, 0:256], AF.Copy)
         V("cp", ["MI2"], ["N1t"], T.N1t[:], T.MI2[:, 0:16])
-        if t > 0:
-            V("cp", ["MI1"], ["AI"], T.AI[:], T.MI1[:, 0:2])
-        absv(0, 0, "A", 0, 64)
+        offsets("PO1", "ODD0", "OA0", 128, 256)
         A([PW, "N1t"], ["L1"], T.L1[:], W[:, 256:512].indirect(T.N1t[:, 0:16]), AF.Copy)
-        pos(1, 1, "PO0")
+        absv(0, 0, "A", 0, 64)
+        for c in range(2):
+            for v in range(2):
+                pos(c, v, "PO0", 256 - NC, 256, T.PO0[:, 2 * c + v:4 * NC:4])
         allowed(0)
         gat(0, 0, "A", 64, 128)
+        offsets("PO0", "ODDC", "OC", 0, 4 * NC)
         allowed(1)
         absv(0, 0, "A", 64, 128)
-        offsets(0, 1, "PO1")
-        offsets(1, 1, "PO0")
-        A([(STn, 0, 256)], [(Wn, 0, 256)], W[:, 0:256], ST[:, 0:256], AF.Copy)
-        pos(1, 0, "PO1")
-        if t == 0:
-            lastconsts()
-        pen(0)
-        q0 = 0
+        for v in range(2):
+            pos(1, v, "PO1", 0, 128, T.PO1[:, 128 * v:128 * v + 128])
+        for c in range(2):
+            for v in range(2):
+                pos(c, v, "PO0", 128, 128 + NB, T.PO0[:, NB * (2 * c + v):NB * (2 * c + v) + NB])
+        V("ts", ["AR"], ["PN"], T.PN[:], T.AR[:], 127.5, None, OP.is_gt)
         keys(0, 0, "A", "KA0")
-        cslots(q0, q0 + CPART[0])
-        q0 += CPART[0]
+        cslots(0, CFIRST)
+        keysc(0, CFIRST)
         gat(0, 1, "A")
         absv(0, 1, "A")
         keys(0, 1, "A", "KA0")
-        offsets(1, 0, "PO1")
-        pen(1)
-        cslots(q0, q0 + CPART[1])
-        q0 += CPART[1]
+        offsets("PO1", "ODD0", "OA1", 0, 256)
+        cslots(CFIRST, NC)
+        keysc(CFIRST, NC)
         gat(1, 0, "A")
         absv(1, 0, "A")
         keys(1, 0, "A", "KA1")
         A(["KA0"], ["K0S0"], T.K0S0[:], T.KA0[:, 0:128], AF.Copy)
-        cslots(q0, q0 + CPART[2])
-        q0 += CPART[2]
         gat(1, 1, "A")
-        V("tt", [x1, n0q], [("DNM", 0, 16)], T.DNM[:, 0:16], n1q, T[n0q][:], OP.subtract)
-        V("tt", [n0q, "IQ"], [("DNM", 16, 32)], T.DNM[:, 16:32], T[n0q][:], T.IQ[:], OP.subtract)
-        if t > 0:
-            V("ts", ["AI"], ["AI"], T.AI[:], T.AI[:], 7, None, OP.bitwise_and)
-        V("ts", [("DNM", 0, 16)], [("DNM", 0, 16)], T.DNM[:, 0:16], T.DNM[:, 0:16], 0.0625, None, OP.mult)
-        if t > 0:
-            V("cp", ["AI"], ["AFl"], T.AFl[:], T.AI[:])
-            for x in range(2):
-                V("ts", ["AFl", "F"], [("FT", 0, 16)], T.FT[:, x:16:2], T.F[:, x:16:2], T.AFl[:, x:x + 1], 32.0, OP.subtract, OP.mult)
+        offsets("PO0", "ODDB", "OB", 0, 4 * NB)
         absv(1, 1, "A")
-        cslots(q0, NC)
-        keysc()
+        A([x1], [("D1", 0, 1)], T.D1[:, 0:80:5], n1q, AF.Copy)
         keys(1, 1, "A", "KA1")
         for v in range(2):
             gat(0, v, "B")
@@ -458,24 +459,39 @@ def rank_program(g, core, T, topo):
         gat(1, 1, "B", 0, NB - NL)
         absv(1, 1, "B", 0, NB - NL)
         gat(1, 1, "B", NB - NL, NB)
-        A(["KA0"], [("K0S1", NB, 128)], T.K0S1[:, NB:128], T.KA0[:, 256:256 + 2 * NC:2], AF.Copy)
         absv(1, 1, "B", NB - NL, NB)
+        A(["KB0"], [("K0S1", NB, 128)], T.K0S1[:, NB:128], T.KB0[:, 256:256 + 2 * NC:2], AF.Copy)
         A(["KB0"], [("K0S1", 0, NB)], T.K0S1[:, 0:NB], T.KB0[:, 0:NB], AF.Copy)
-        V("tt", ["KA0", ("K0S1", NB, 128)], [("km1", NB, 128)], T.km1[:, NB:128], T.KA0[:, 257:256 + 2 * NC:2], T.K0S1[:, NB:128], OP.min)
         keys(1, 1, "B", "KB1")
+        if t == 0:
+            lastconsts()
+            n0steps(T[n0q][:], [n0q])
         best(0)
+        V("tt", ["KB0", ("K0S1", NB, 128)], [("km1", NB, 128)], T.km1[:, NB:128], T.KB0[:, 257:256 + 2 * NC:2], T.K0S1[:, NB:128], OP.min)
+        site(0, 0)
+        site(0, 1)
         best(1)
         accept()
         if t < 3:
             sn = "ST%d" % (t + 1)
             newsrc()
             newlists(T[sn][:, 0:256], [(sn, 0, 256)])
+            wn = "W%d" % (t + 1)
+            A([(sn, 0, 256)], [(wn, 0, 256)], T[wn][:, 0:256], T[sn][:, 0:256], AF.Copy)
             send(t + 1, T.cores[(rank - 1 - (t + 1) % (NR_ - 1)) % NR_])
             newnx(T[m0][:], [m0])
             swap("MI1", lambda x: T[m0][:, x:16:2], [m0])
             newf(T.F[:], ["F"])
+            V("tt", [("D0", 4, 5), "AS"], ["AS"], T.AS[:], acc, T.AS[:], OP.add)
+            for b in range(8):
+                mm(["B32", "AS"], ["MI2"], T.MI2[:, 0:2], T.B32[:], T.AS[:, 2 * b:2 * b + 2], b == 0, b == 7)
             V("cp", ["MI1"], [mt], T[mt][:], T.MI1[:, 0:16])
-            V("tt", [rf(0), "AS"], ["AS"], T.AS[:], F_(0), T.AS[:], OP.add)
+            n0steps(T[m0][:], [m0])
+            V("cp", ["MI2"], ["AI"], T.AI[:], T.MI2[:, 0:2])
+            V("ts", ["AI"], ["AI"], T.AI[:], T.AI[:], 7, None, OP.bitwise_and)
+            V("cp", ["AI"], ["AFl"], T.AFl[:], T.AI[:])
+            for x in range(2):
+                V("ts", ["AFl", "F"], [("FT", x, x + 1)], T.FT[:, x:16:2], T.F[:, x:16:2], T.AFl[:, x:x + 1], 32.0, OP.subtract, OP.mult)
         else:
             newnx(T.ZO[:, 1:256:16], [("ZO", 1, 2)])
             newf(T.ZO[:, 0:256:16], [("ZO", 0, 1)])

from concourse.mybir import AluOpType as OP, AxisListType, ActivationFunctionType as AF

NC = 48
NB = 128 - NC
CFIRST = 24
NL = 32
BIG = float(2 ** 26)

SCRATCH = {
    "S": ("sbuf", [128, 4096], "bfloat16"), "X": ("sbuf", [128, 256], "bfloat16"),
    "XE": ("sbuf", [128, 16 * (128 + NB)], "bfloat16"),
    "RI": ("sbuf", [128, 256], "int32"), "SI": ("sbuf", [128, 16], "int32"), "NI": ("sbuf", [128, 16], "int32"),
    "FI": ("sbuf", [128, 256], "int32"), "FF": ("sbuf", [128, 512], "float32"),
    "F": ("sbuf", [128, 16], "float32"), "FT": ("sbuf", [128, 16], "float32"),
    "SN": ("sbuf", [128, 32], "bfloat16"),
    "ip": ("sbuf", [128, 1], "int32"), "ic": ("sbuf", [128, 8], "int32"), "CF": ("sbuf", [128, 8], "float32"),
    "dm": ("sbuf", [128, 128], "bfloat16"), "jm1": ("sbuf", [128, 128], "bfloat16"), "jb": ("sbuf", [128, 128], "bfloat16"),
    "gm": ("sbuf", [128, 128], "bfloat16"), "gm2": ("sbuf", [128, 128], "bfloat16"), "jw": ("sbuf", [128, 256], "bfloat16"),
    "JK": ("sbuf", [128, 384], "bfloat16"), "ODD0": ("sbuf", [128, 256], "float32"), "ODDB": ("sbuf", [128, 4 * NB], "float32"), "ODDC": ("sbuf", [128, 4 * NC], "float32"),
    "IQ": ("sbuf", [128, 16], "float32"),
    "SW": ("sbuf", [128, 512], "bfloat16"), "B": ("sbuf", [128, 128], "bfloat16"), "B32": ("sbuf", [128, 128], "bfloat16"),
    "BX": ("sbuf", [128, 128], "bfloat16"), "JA": ("sbuf", [128, 128], "bfloat16"), "JB": ("sbuf", [128, 128], "bfloat16"),
    "TRI": ("sbuf", [128, 128], "bfloat16"), "HN": ("sbuf", [128, 128], "bfloat16"), "I": ("sbuf", [128, 128], "bfloat16"),
    "IB": ("sbuf", [128, 128], "bfloat16"), "NBM": ("sbuf", [128, 128], "bfloat16"), "P22": ("sbuf", [128, 128], "bfloat16"),
    "LG": ("sbuf", [128, 15 * 128], "bfloat16"), "LH": ("sbuf", [128, 16 * 128], "bfloat16"),
    "J16": ("sbuf", [128, 128], "bfloat16"), "ones": ("sbuf", [128, 256], "bfloat16"),
    "KM": ("sbuf", [128, 256], "bfloat16"), "RS": ("sbuf", [128, 128], "float32"),
    "XS": ("sbuf", [128, 256], "bfloat16"), "SR": ("sbuf", [128, 256], "bfloat16"), "NR": ("sbuf", [128, 256], "bfloat16"),
    "D0": ("sbuf", [128, 80], "int32"), "D1": ("sbuf", [128, 80], "float32"), "FS": ("sbuf", [128, 80], "bfloat16"), "SEL": ("sbuf", [128, 16], "uint16"), "EX": ("sbuf", [128, 16], "uint16"),
    "AI": ("sbuf", [128, 2], "int32"), "AFl": ("sbuf", [128, 2], "float32"), "AS": ("sbuf", [128, 16], "bfloat16"),
    "AR": ("sbuf", [128, 512], "bfloat16"), "PN": ("sbuf", [128, 512], "bfloat16"),
    "L0": ("sbuf", [128, 256], "bfloat16"), "L1": ("sbuf", [128, 256], "bfloat16"), "N1t": ("sbuf", [128, 16], "uint16"),
    "OC": ("sbuf", [128, 4 * NC], "uint16"), "CD": ("sbuf", [128, 64 * NC], "bfloat16"),
    "TI": ("sbuf", [128, 48], "int32"), "TF": ("sbuf", [128, 112], "float32"),
    "IBo": ("sbuf", [128, 4 * NB], "int32"), "IC": ("sbuf", [128, 4 * NC], "int32"), "OB": ("sbuf", [128, 4 * NB], "uint16"),
    "KA0": ("psum", [128, 512], "float32"), "KA1": ("psum", [128, 512], "float32"),
    "KB0": ("psum", [128, 512], "float32"), "KB1": ("psum", [128, 512], "float32"),
    "PO0": ("psum", [128, 512], "float32"), "PO1": ("psum", [128, 512], "float32"),
    "MI1": ("psum", [128, 512], "float32"), "MI2": ("psum", [128, 512], "float32"),
}
for _t in range(4):
    SCRATCH["W%d" % _t] = ("sbuf", [128, 528], "bfloat16")
    SCRATCH["ST%d" % _t] = ("sbuf", [128, 272], "bfloat16")
for _c in range(2):
    SCRATCH["N0t%d" % _c] = ("sbuf", [128, 16], "uint16")
    SCRATCH["N0q%d" % _c] = ("sbuf", [128, 16], "bfloat16")
    SCRATCH["X1%d" % _c] = ("sbuf", [128, 256], "bfloat16")
    SCRATCH["OA%d" % _c] = ("sbuf", [128, 256], "uint16")
    SCRATCH["IA%d" % _c] = ("sbuf", [128, 256], "int32")
    for _v in range(2):
        SCRATCH["DA%d%d" % (_c, _v)] = ("sbuf", [128, 2048], "bfloat16")
        SCRATCH["DB%d%d" % (_c, _v)] = ("sbuf", [128, 16 * NB], "bfloat16")
    for _n in ("K0S", "km", "XT"):
        SCRATCH[_n + str(_c)] = ("sbuf", [128, 128], "float32")
for _n in ("OUT", "ZO", "ZR"):
    SCRATCH[_n] = ("sbuf", [128, 256], "float32")
SCRATCH["Y"] = ("sbuf", [128, 256], "int32")
for _n in ("CR", "CT", "OH", "BS", "MD"):
    SCRATCH[_n] = ("sbuf", [128, 256], "bfloat16")
SCRATCH["ZC"] = ("sbuf", [128, 256], "int32")

NDMA = 16
SEMAPHORES = ["sV", "sA", "sP", "sG", "sL"] + ["d%d" % k for k in range(NDMA)] + ["arr%d" % k for k in range(4)]
PSUM = ("KA0", "KA1", "KB0", "KB1", "PO0", "PO1", "MI1", "MI2")


def rank_program(g, core, T, topo):
    rank = T.rank_of(core)
    if rank is None:
        return
    NR_ = len(T.cores)
    queues = {"V": g.vector, "A": g.scalar, "P": g.tensor, "G": g, "S": g.sync}

    ops, last, ndma, sent, compn = [], {}, [0], [0], {}

    def norm(x):
        if isinstance(x, str):
            return (x, 0, 1 << 30)
        return x

    def op(q, fn, r=(), w=(), comp=None, amt=1):
        me = len(ops)
        deps = set()
        rr, ww = [norm(x) for x in r], [norm(x) for x in w]
        for name, a, b in rr:
            for (a2, b2, o, iw) in last.get(name, []):
                if name in PSUM:
                    if ops[o]["q"] != q:
                        deps.add(o)
                elif iw and a < b2 and a2 < b:
                    deps.add(o)
        for name, a, b in ww:
            for (a2, b2, o, iw) in last.get(name, []):
                if name in PSUM:
                    if ops[o]["q"] != q or q != "P":
                        deps.add(o)
                elif a < b2 and a2 < b:
                    deps.add(o)
        for name, a, b in ww:
            ps = name in PSUM
            last[name] = [e for e in last.get(name, []) if not (ps or (a <= e[0] and e[1] <= b))] + [(a, b, me, True)]
        for name, a, b in rr:
            last.setdefault(name, []).append((a, b, me, False))
        comp = comp or q
        ci = compn.get(comp, 0)
        compn[comp] = ci + 1
        deps.discard(me)
        ops.append({"q": q, "fn": fn, "deps": deps, "comp": comp, "ci": ci, "amt": amt, "sig": amt != 1, "need": []})

    def dma(q, out, in_, r=(), w=()):
        k = ndma[0]
        ndma[0] += 1
        qq = queues[q]
        op(q, lambda: qq.dma_start(out, in_), r, w, "d%d" % k, 16)

    def V(name, r, w, *a, **k):
        fn = {"tt": g.vector.tensor_tensor, "ts": g.vector.tensor_scalar, "cp": g.vector.tensor_copy, "tr": g.vector.transpose,
              "scan": g.vector.tensor_tensor_scan, "set": g.vector.memset}[name]
        op("V", lambda: fn(*a, **k), r, w)

    def A(r, w, out, in_, func, **k):
        op("A", lambda: g.scalar.activation(out, in_, func, **k), r, w)

    def mm(r, w, out, lhsT, rhs, start, stop):
        op("P", lambda: g.tensor.matmul(out, lhsT, rhs, start, stop), r, w)

    def iota(w, out, pattern, base, cm, small=True):
        if small:
            op("G", lambda: g.iota(out, pattern, base, cm, allow_small_or_imprecise_dtypes=True), (), w)
        else:
            op("G", lambda: g.iota(out, pattern, base, cm), (), w)

    def swap(bank, ap, r):
        for y in range(2):
            for x in range(2):
                mm(["SW"] + r, [bank], T[bank][:, y:16:2], T.SW[:, 128 * (2 * y + x):128 * (2 * y + x) + 128], ap(x), x == 0, x == 1)

    def send(t, dst):
        rid, pid, _ = topo.addr(dst)
        m = topo.mask(core, dst)
        sent[0] += len(topo.engines(core, dst))
        out, src = T["W%d" % t][:, 256:528], T["ST%d" % t][:]
        op("G", lambda: g.remote_dma(out, src, T.sem["arr%d" % t], T.sem.sL, pid, rid, m), ["ST%d" % t], (), "sL", 0)

    def recv(t, src):
        op("N", None, (), [("W%d" % t, 256, 528)], "arr%d" % t, len(topo.engines(src, core)))

    dma("S", T.RI[:], T.resid[:], (), ["RI"])
    dma("A", T.SI[:], T.src0[:], (), ["SI"])
    dma("S", T.NI[:], T.nx0[:], (), ["NI"])
    dma("A", T.X[:], T.obs[:], (), ["X"])
    dma("S", T.S[:, 0:2048], T.prof[:, 0:2048], (), [("S", 0, 2048)])
    dma("A", T.S[:, 2048:4096], T.prof[:, 2048:4096], (), [("S", 2048, 4096)])

    iota(["ip"], T.ip[:], [[0, 1]], 0, 1, False)
    iota(["dm"], T.dm[:], [[1, 128]], 0, -1)
    V("set", (), ["FI"], T.FI[:], 0)
    dma("S", T.FI[0:128:16, :], T.fit0[:], (), ["FI"])
    iota(["gm"], T.gm[:], [[1, 8], [0, 16]], 0, 0)
    iota(["jm1"], T.jm1[:], [[0, 8], [1, 16]], 1, 0)
    iota(["jb"], T.jb[:], [[0, 8], [1, 16]], -20, 0)
    iota(["jw"], T.jw[:], [[0, 16], [1, 16]], 0, 0)
    V("ts", ["ip"], [("ic", 0, 1)], T.ic[:, 0:1], T.ip[:], 15, None, OP.bitwise_and)
    V("ts", ["ip"], [("ic", 1, 2)], T.ic[:, 1:2], T.ip[:], 4, None, OP.arith_shift_right)
    V("ts", ["ip"], [("ic", 2, 3)], T.ic[:, 2:3], T.ip[:], 4, 1, OP.arith_shift_right, OP.bitwise_and)
    V("ts", ["ip"], [("ic", 3, 4)], T.ic[:, 3:4], T.ip[:], 31, None, OP.bitwise_and)
    V("ts", ["ip"], [("ic", 4, 5)], T.ic[:, 4:5], T.ip[:], 5, None, OP.arith_shift_right)

    def col(k, s, m, a):
        V("ts", [("ic", s, s + 1)], [("CF", k, k + 1)], T.CF[:, k:k + 1], T.ic[:, s:s + 1], float(m), float(a), OP.mult, OP.add)

    def C(k):
        return T.CF[:, k:k + 1]
    col(3, 2, 1, 0)
    col(4, 2, -1, 1)
    col(0, 0, 1, 1)
    col(1, 0, 1, -20)
    col(2, 1, 1, 0)
    col(5, 0, 1, 0)
    col(6, 3, 1, 0)
    col(7, 4, 1, 0)
    for y in range(2):
        for x in range(2):
            s = 128 * (2 * y + x)
            V("ts", ["dm", ("CF", 3, 5)], [("SW", s, s + 128)], T.SW[:, s:s + 128], T.dm[:], float(16 * (x - y)), C(3 if y else 4),
              OP.is_equal, OP.mult)
    V("cp", ["SI"], [("SN", 0, 16)], T.SN[:, 0:16], T.SI[:])
    V("cp", ["NI"], [("SN", 16, 32)], T.SN[:, 16:32], T.NI[:])
    V("cp", ["NI"], ["N0t0"], T.N0t0[:], T.NI[:])
    V("cp", ["RI"], [("ST0", 0, 256)], T.ST0[:, 0:256], T.RI[:])
    swap("MI1", lambda x: T.SN[:, x:16:2], [("SN", 0, 16)])
    V("cp", ["MI1"], [("ST0", 256, 272)], T.ST0[:, 256:272], T.MI1[:, 0:16])
    send(0, T.cores[(rank - 1) % NR_])
    swap("MI2", lambda x: T.SN[:, 16 + x:32:2], [("SN", 16, 32)])
    V("cp", ["MI2"], ["N0q0"], T.N0q0[:], T.MI2[:, 0:16])
    iota(["ODD0"], T.ODD0[:], [[0, 2], [2, 128]], 1, 0)
    NX = 128 + NB
    for k in range(16):
        A(["X"], [("XEk", k, k + 1)], T.XE[:, k:16 * NX:16], T.X[:, 0:NX], AF.Copy)
    V("set", (), ["ones"], T.ones[:], 1.0)
    V("set", (), [("JK", 256, 384)], T.JK[0:1, 256:384], 4096.0)
    V("set", (), ["J16"], T.J16[0:1, :], 16.0)
    V("cp", ["jw"], ["EX"], T.EX[:], T.jw[:, 0:16])
    V("ts", ["jw"], ["KM"], T.KM[:], T.jw[:], 0.0, None, OP.is_gt)
    V("ts", ["gm", "CF"], ["B"], T.B[:], T.gm[:], C(2), None, OP.is_equal)
    V("ts", ["B"], ["BX"], T.BX[:], T.B[:], 32.0, None, OP.mult)
    V("tt", ["jm1", "B"], ["JA"], T.JA[:], T.jm1[:], T.B[:], OP.mult)
    V("tt", ["jb", "B"], ["JB"], T.JB[:], T.jb[:], T.B[:], OP.mult)
    V("ts", ["JA", "CF"], ["TRI"], T.TRI[:], T.JA[:], C(0), None, OP.is_ge)
    V("ts", ["JB", "CF"], ["HN"], T.HN[:], T.JB[:], C(1), -1.0, OP.is_lt, OP.mult)
    V("ts", ["JA", "CF"], ["I"], T.I[:], T.JA[:], C(0), None, OP.is_equal)
    V("tt", ["I", "B"], ["IB"], T.IB[:], T.I[:], T.B[:], OP.subtract)
    V("ts", ["B"], ["NBM"], T.NBM[:], T.B[:], -1.0, None, OP.mult)
    V("ts", ["I"], ["P22"], T.P22[:], T.I[:], float(2 ** 22), None, OP.mult)
    V("ts", ["jw"], ["RS"], T.RS[:], T.jw[:, 0:128], 0.0, BIG, OP.is_equal, OP.mult)
    for k in range(4):
        V("ts", ["JA"], [("LG", k, k + 1)], T.LG[:, 128 * k:128 * k + 128], T.JA[:], float(k + 1), 32.0, OP.is_gt, OP.mult)

    def step(name, k, base, m):
        out = T[name][:, 128 * k:128 * k + 128]
        op("G", lambda: g.affine_select(out, T.BX[:], [[0, 8], [m, 16]], OP.is_ge, 0.0, base, 0), ["BX"], [(name, k, k + 1)])
    for k in range(4, 15):
        step("LG", k, -k - 1, 1)
    iota(["ODDC"], T.ODDC[:], [[2, NC], [0, 4]], 257 + 2 * NB, 0)
    iota([("JK", 0, 256)], T.JK[0:1, 0:256], [[16, 2], [0, 8], [1, 16]], 0, 0)
    for k in range(16):
        step("LH", k, k, -1)
    iota(["ODDB"], T.ODDB[:], [[0, 4], [2, NB]], 257, 0)
    iota(["IQ"], T.IQ[:], [[32, 8], [0, 2]], -256, 0)
    iota(["gm2"], T.gm2[:], [[1, 4], [0, 32]], 0, 0)

    def lastconsts():
        V("cp", ["FI"], [("FF", 0, 256)], T.FF[:, 0:256], T.FI[:])
        V("tr", [("FF", 0, 256)], [("FF", 256, 512)], T.FF[:, 256:512], T.FF[:, 0:256])
        V("cp", [("FF", 256, 512)], ["F"], T.F[:], T.FF[:, 256:512:16])
        V("ts", ["F"], ["FT"], T.FT[:], T.F[:], 32.0, None, OP.mult)
        V("ts", ["IQ", "CF"], ["IQ"], T.IQ[:], T.IQ[:], C(6), None, OP.add)
        V("ts", ["gm2", "CF"], ["B32"], T.B32[:], T.gm2[:], C(7), None, OP.is_equal)
        V("set", (), ["AS"], T.AS[:], 0.0)
        V("set", (), ["ZC"], T.ZC[:], 0)
        V("set", (), ["D0"], T.D0[:], 0)
        for k in (1, 3):
            V("ts", ["IQ"], [("D0", k, k + 1)], T.D0[:, k:80:5], T.IQ[:], 0.0, 1.0, OP.mult, OP.add)
        V("ts", ["IQ"], [("D1", 3, 4)], T.D1[:, 3:80:5], T.IQ[:], -1.0, None, OP.mult)
        V("cp", ["IQ"], [("D1", 4, 5)], T.D1[:, 4:80:5], T.IQ[:])
        V("set", (), ["ZO"], T.ZO[:], 0.0)

    for t in range(4):
        par = t & 1
        W, Wn = T["W%d" % t], "W%d" % t
        ST, STn = T["ST%d" % t], "ST%d" % t
        n0t, n0q, x1 = "N0t%d" % par, "N0q%d" % par, "X1%d" % par
        m0, mt = "N0q%d" % (1 - par), "N0t%d" % (1 - par)
        n1q = T[x1][:, 0:256:16]
        recv(t, T.cores[(rank + 1 + t % (NR_ - 1)) % NR_])

        def pos0(v, bank, a, b, o):
            mm([("JK", 256, 384), "ones"], [bank], o, T.JK[0:1, 256:384], T.ones[0:1, 0:b - a], True, False)
            if v:
                mm(["B", ("ST0", 0, 256)], [bank], o, T.B[:], T.ST0[:, a:b], False, False)

        def pos1(c, v, bank, a, b, o):
            m = "HN" if v else "TRI"
            mm([m, ("L%d" % c, a, b)], [bank], o, T[m][:], T["L%d" % c][:, a:b], False, True)

        def pos(c, v, bank, a, b, o):
            pos0(v, bank, a, b, o)
            pos1(c, v, bank, a, b, o)

        def allowed(c):
            mm(["B", ("ST0", 0, 256)], ["MI1"], T.MI1[:, 0:256], T.B[:], T.ST0[:, 0:256], True, False)
            mm(["IB", "L%d" % c], ["MI1"], T.MI1[:, 0:256], T.IB[:], T["L%d" % c][:, 0:256], False, True)
            A(["MI1"], [("AR", c, c + 1)], T.AR[:, 256 * c:256 * c + 256], T.MI1[:, 0:256], AF.Abs, bias=-127.5)

        def offsets(bank, odd, o, a, b):
            In = "IBo" if o == "OB" else "I" + o[1:]
            ib = T[In][:, a:b]
            V("tt", [bank, odd], [(In, a, b)], ib, T[bank][:, 0:b - a], T[odd][:, 0:b - a], OP.mult)
            V("ts", [(In, a, b)], [(In, a, b)], ib, ib, 2, 4095, OP.arith_shift_right, OP.bitwise_and)
            V("cp", [(In, a, b)], [(o, a, b)], T[o][:, a:b], ib)

        def gat(c, v, s, n0=0, n1=None):
            d = "D%s%d%d" % (s, c, v)
            o, k = ("OA%d" % c, 128 * v) if s == "A" else ("OB", NB * (2 * c + v))
            n1 = (128 if s == "A" else NB) if n1 is None else n1
            xb = 0 if s == "A" else 2048
            V("tt", ["S", "XEk", (o, k + n0, k + n1)], [(d, 16 * n0, 16 * n1)], T[d][:, 16 * n0:16 * n1],
              T.S[:, 0:4096].indirect(T[o][:, k + n0:k + n1]), T.XE[:, xb + 16 * n0:xb + 16 * n1], OP.subtract)

        def absv(c, v, s, n0=0, n1=None):
            d = "D%s%d%d" % (s, c, v)
            n1 = (128 if s == "A" else NB) if n1 is None else n1
            A([(d, 16 * n0, 16 * n1)], [(d, 16 * n0, 16 * n1)], T[d][:, 16 * n0:16 * n1], T[d][:, 16 * n0:16 * n1], AF.Abs)

        def keystart(c, bank, a, b, sl):
            mm([("JK", 0, 256), "ones"], [bank], T[bank][:, a:b], T.JK[0:1, 128 * c:128 * c + 128], T.ones[0:1, 0:b - a], True, False)
            mm(["P22", "PN"], [bank], T[bank][:, a:b], T.P22[:], T.PN[:, 256 * c + sl:256 * c + sl + b - a], False, False)

        def keys(c, v, s, bank):
            d = "D%s%d%d" % (s, c, v)
            n = 128 if s == "A" else NB
            if v == 0:
                keystart(c, bank, 0, n, 0 if s == "A" else 128)
            for k in range(15 + v):
                l = "LH" if v else "LG"
                mm([(l, k, k + 1), d], [bank], T[bank][:, 0:n], T[l][:, 128 * k:128 * k + 128], T[d][:, k:16 * n:16], False, v == 1 and k == 15)

        def cslots(a, b):
            for s in range(a, b):
                i = 256 - NC + s
                A(["S", "OC", "X"], [("CD", s, s + 1)], T.CD[:, 64 * s:64 * s + 64], T.S[:, 0:4096].indirect(T.OC[:, 4 * s:4 * s + 4]), AF.Abs,
                  bias=T.X[:, i:i + 1], scale=-1.0)

        def keysc(s0, s1):
            n, o = s1 - s0, T.KB0[:, 256 + 2 * s0:256 + 2 * s1]
            mm([("JK", 0, 256), "ones"], ["KB0"], o, T.JK[0:1, 0:128], T.ones[0:1, 0:2 * n], True, False)
            mm(["J16", "ones"], ["KB0"], T.KB0[:, 257 + 2 * s0:256 + 2 * s1:2], T.J16[0:1, :], T.ones[0:1, 0:n], False, False)
            for c in range(2):
                i = 256 * c + 256 - NC
                mm(["P22", "PN"], ["KB0"], T.KB0[:, 256 + 2 * s0 + c:256 + 2 * s1:2], T.P22[:], T.PN[:, i + s0:i + s1], False, False)
            for v in range(2):
                l = "LH" if v else "LG"
                for k in range(15 + v):
                    mm([(l, k, k + 1), ("CD", s0, s1)], ["KB0"], o, T[l][:, 128 * k:128 * k + 128],
                       T.CD[:, 64 * s0 + 16 * v + k:64 * s1:32], False, v == 1 and k == 15)

        def I_(k):
            return T.TI[:, 16 * k:16 * k + 16]

        def F_(k):
            return T.TF[:, 16 * k:16 * k + 16]

        def ri(k):
            return ("TI", k, k + 1)

        def rf(k):
            return ("TF", k, k + 1)
        key, acc, nsel = T.Y[:, 15:256:16], T.D0[:, 4:80:5], T.FS[:, 2:80:5]

        def n0steps(n, r):
            V("ts", r, [("D1", 1, 2)], T.D1[:, 1:80:5], n, -1.0, None, OP.mult)
            V("cp", r, [("D1", 2, 3)], T.D1[:, 2:80:5], n)

        def best(h):
            x, a, b = str(h), 128 * h, 128 * h + 128
            k1 = "KA1" if h == 0 else "KB1"
            n = 128 if h == 0 else NB
            V("tt", [k1, ("K0S" + x, 0, n)], [("km" + x, 0, n)], T["km" + x][:, 0:n], T[k1][:, 0:n], T["K0S" + x][:, 0:n], OP.min)
            V("tr", ["km" + x], ["XT" + x], T["XT" + x][:], T["km" + x][:])
            V("scan", ["RS", "XT" + x], [("Y", a, b)], T.Y[:, a:b], T.RS[:], T["XT" + x][:], BIG, OP.add, OP.min)

        def site(h, part):
            a, b = 128 * h, 128 * h + 128
            if part == 0:
                V("ts", [("Y", a, b)], [("ZC", a, b)], T.ZC[:, a:b:16], T.Y[:, a + 15:b:16], 15, None, OP.bitwise_and)
                V("scan", ["KM", ("ZC", a, b)], [("CR", a, b)], T.CR[:, a:b], T.KM[:, a:b], T.ZC[:, a:b], 0.0, OP.mult, OP.add)
                V("tr", [("CR", a, b)], [("CT", a, b)], T.CT[:, a:b], T.CR[:, a:b])
            else:
                V("ts", [("CT", a, b), "CF"], [("OH", a, b)], T.OH[:, a:b], T.CT[:, a:b], C(5), None, OP.is_equal)

        def accept():
            V("ts", ["Y"], [("D0", 2, 3)], T.D0[:, 2:80:5], key, 4, 1, OP.arith_shift_right, OP.bitwise_and)
            V("tt", ["Y", "FT"], [("D0", 4, 5)], acc, key, T.FT[:], OP.is_lt)
            V("scan", ["D0", "D1"], ["FS"], T.FS[:], T.D0[:], T.D1[:], 0.0, OP.mult, OP.add)
            swap("MI2", lambda x: T.FS[:, 4 + 5 * x:80:10], ["FS"])
            site(1, 0)
            V("ts", ["MI2"], ["SEL"], T.SEL[:], T.MI2[:, 0:16], 256.0, None, OP.add)
            mm(["B", ("ST0", 0, 256)], ["MI1"], T.MI1[:, 0:256], T.B[:], T.ST0[:, 0:256], True, False)
            V("cp", [(Wn, 0, 512), "SEL"], ["BS"], T.BS[:], W[:, 0:512].indirect(T.SEL[:, 0:16]))
            mm(["NBM", "BS"], ["MI1"], T.MI1[:, 0:256], T.NBM[:], T.BS[:], False, True)
            mm(["I", "BS"], ["MI2"], T.MI2[:, 0:256], T.I[:], T.BS[:], True, True)
            site(1, 1)

        def newlists(out, w):
            V("tt", ["MI1", "OH"], ["MD"], T.MD[:], T.MI1[:, 0:256], T.OH[:], OP.mult)
            V("tt", ["MI2", "MD"], w, out, T.MI2[:, 0:256], T.MD[:], OP.add)

        def newsrc():
            sn = "ST%d" % (t + 1)
            so, wo = ST[:, 256:272], (STn, 256, 272)
            V("tt", ["FS", wo], [rf(0)], F_(0), nsel, so, OP.subtract)
            V("tt", [rf(0), ("D0", 4, 5)], [rf(1)], F_(1), F_(0), acc, OP.mult)
            V("tt", [rf(1), wo], [(sn, 256, 272)], T[sn][:, 256:272], F_(1), so, OP.add)

        def newnx(out, w):
            V("ts", ["FS"], [rf(2)], F_(2), nsel, 416.0, None, OP.mult)
            V("tt", [rf(2), "Y"], [ri(0)], I_(0), F_(2), key, OP.add)
            V("ts", [ri(0)], [ri(1)], I_(1), I_(0), 5, 255, OP.arith_shift_right, OP.bitwise_and)
            V("tt", [ri(1), x1], [rf(3)], F_(3), I_(1), n1q, OP.subtract)
            V("tt", [rf(3), ("D0", 4, 5)], [rf(4)], F_(4), F_(3), acc, OP.mult)
            V("tt", [rf(4), x1], w, out, F_(4), n1q, OP.add)

        def newf(out, w):
            V("ts", ["Y"], [ri(2)], I_(2), key, 5, None, OP.arith_shift_right)
            V("tt", [ri(2), "F"], [rf(5)], F_(5), I_(2), T.F[:], OP.subtract)
            V("tt", [rf(5), ("D0", 4, 5)], [rf(6)], F_(6), F_(5), acc, OP.mult)
            V("tt", [rf(6), "F"], w, out, F_(6), T.F[:], OP.add)

        PW = (Wn, 256, 512)
        V("cp", [PW, n0t], [("L0", 0, 128)], T.L0[:, 0:128], W[:, 256:512].indirect(T[n0t][:, 0:8]))
        A([(Wn, 512, 528), "EX"], ["XS"], T.XS[:], W[:, 512:528].indirect(T.EX[:, 0:16]), AF.Copy)
        oA = T.PO0[:, 0:128]
        pos0(0, "PO0", 0, 128, oA)
        pos0(1, "PO1", 0, 128, T.PO1[:, 0:128])
        pos1(0, 0, "PO0", 0, 128, oA)
        pos1(0, 1, "PO1", 0, 128, T.PO1[:, 0:128])
        V("tr", ["XS"], ["SR"], T.SR[:], T.XS[:])
        A(["SR", n0t], ["NR"], T.NR[:], T.SR[:, 0:256].indirect(T[n0t][:, 0:16]), AF.Copy)
        A([PW, n0t], [("L0", 128, 256)], T.L0[:, 128:256], W[:, 256:512].indirect(T[n0t][:, 8:16]), AF.Copy)
        offsets("PO0", "ODD0", "OA0", 0, 128)
        V("tr", ["NR"], [x1], T[x1][:], T.NR[:])
        gat(0, 0, "A", 0, 64)
        swap("MI2", lambda x: T[x1][:, 16 * x:256:32], [x1])
        if t == 0:
            A([(STn, 0, 256)], [(Wn, 0, 256)], W[:, 0:256], ST[:, 0:256], AF.Copy)
        V("cp", ["MI2"], ["N1t"], T.N1t[:], T.MI2[:, 0:16])
        offsets("PO1", "ODD0", "OA0", 128, 256)
        A([PW, "N1t"], ["L1"], T.L1[:], W[:, 256:512].indirect(T.N1t[:, 0:16]), AF.Copy)
        absv(0, 0, "A", 0, 64)
        for c in range(2):
            for v in range(2):
                pos(c, v, "PO0", 256 - NC, 256, T.PO0[:, 2 * c + v:4 * NC:4])
        allowed(0)
        gat(0, 0, "A", 64, 128)
        offsets("PO0", "ODDC", "OC", 0, 4 * NC)
        allowed(1)
        absv(0, 0, "A", 64, 128)
        for v in range(2):
            pos(1, v, "PO1", 0, 128, T.PO1[:, 128 * v:128 * v + 128])
        for c in range(2):
            for v in range(2):
                pos(c, v, "PO0", 128, 128 + NB, T.PO0[:, NB * (2 * c + v):NB * (2 * c + v) + NB])
        V("ts", ["AR"], ["PN"], T.PN[:], T.AR[:], 127.5, None, OP.is_gt)
        keys(0, 0, "A", "KA0")
        cslots(0, CFIRST)
        keysc(0, CFIRST)
        gat(0, 1, "A")
        absv(0, 1, "A")
        keys(0, 1, "A", "KA0")
        offsets("PO1", "ODD0", "OA1", 0, 256)
        cslots(CFIRST, NC)
        keysc(CFIRST, NC)
        gat(1, 0, "A")
        absv(1, 0, "A")
        keys(1, 0, "A", "KA1")
        A(["KA0"], ["K0S0"], T.K0S0[:], T.KA0[:, 0:128], AF.Copy)
        gat(1, 1, "A")
        offsets("PO0", "ODDB", "OB", 0, 4 * NB)
        absv(1, 1, "A")
        A([x1], [("D1", 0, 1)], T.D1[:, 0:80:5], n1q, AF.Copy)
        keys(1, 1, "A", "KA1")
        for v in range(2):
            gat(0, v, "B")
            absv(0, v, "B")
            keys(0, v, "B", "KB0")
        gat(1, 0, "B")
        absv(1, 0, "B")
        keys(1, 0, "B", "KB1")
        gat(1, 1, "B", 0, NB - NL)
        absv(1, 1, "B", 0, NB - NL)
        gat(1, 1, "B", NB - NL, NB)
        absv(1, 1, "B", NB - NL, NB)
        A(["KB0"], [("K0S1", NB, 128)], T.K0S1[:, NB:128], T.KB0[:, 256:256 + 2 * NC:2], AF.Copy)
        A(["KB0"], [("K0S1", 0, NB)], T.K0S1[:, 0:NB], T.KB0[:, 0:NB], AF.Copy)
        keys(1, 1, "B", "KB1")
        if t == 0:
            lastconsts()
            n0steps(T[n0q][:], [n0q])
        best(0)
        V("tt", ["KB0", ("K0S1", NB, 128)], [("km1", NB, 128)], T.km1[:, NB:128], T.KB0[:, 257:256 + 2 * NC:2], T.K0S1[:, NB:128], OP.min)
        site(0, 0)
        site(0, 1)
        best(1)
        accept()
        if t < 3:
            sn = "ST%d" % (t + 1)
            newsrc()
            newlists(T[sn][:, 0:256], [(sn, 0, 256)])
            wn = "W%d" % (t + 1)
            A([(sn, 0, 256)], [(wn, 0, 256)], T[wn][:, 0:256], T[sn][:, 0:256], AF.Copy)
            send(t + 1, T.cores[(rank - 1 - (t + 1) % (NR_ - 1)) % NR_])
            newnx(T[m0][:], [m0])
            swap("MI1", lambda x: T[m0][:, x:16:2], [m0])
            newf(T.F[:], ["F"])
            V("tt", [("D0", 4, 5), "AS"], ["AS"], T.AS[:], acc, T.AS[:], OP.add)
            for b in range(8):
                mm(["B32", "AS"], ["MI2"], T.MI2[:, 0:2], T.B32[:], T.AS[:, 2 * b:2 * b + 2], b == 0, b == 7)
            V("cp", ["MI1"], [mt], T[mt][:], T.MI1[:, 0:16])
            n0steps(T[m0][:], [m0])
            V("cp", ["MI2"], ["AI"], T.AI[:], T.MI2[:, 0:2])
            V("ts", ["AI"], ["AI"], T.AI[:], T.AI[:], 7, None, OP.bitwise_and)
            V("cp", ["AI"], ["AFl"], T.AFl[:], T.AI[:])
            for x in range(2):
                V("ts", ["AFl", "F"], [("FT", x, x + 1)], T.FT[:, x:16:2], T.F[:, x:16:2], T.AFl[:, x:x + 1], 32.0, OP.subtract, OP.mult)
        else:
            newnx(T.ZO[:, 1:256:16], [("ZO", 1, 2)])
            newf(T.ZO[:, 0:256:16], [("ZO", 0, 1)])
            newlists(T.OUT[:], ["OUT"])
            dma("S", T.yr[:], T.OUT[:], ["OUT"], ())
            V("tr", ["ZO"], ["ZR"], T.ZR[:], T.ZO[:])
            dma("A", T.yf[:], T.ZR[0:128:16, :], ["ZR"], ())
            dma("S", T.yn[:], T.ZR[1:128:16, :], ["ZR"], ())

    known = {}
    for o in ops:
        kn = known.setdefault(o["q"], {}) if o["q"] != "N" else {}
        for d in sorted(o["deps"], reverse=True):
            p = ops[d]
            if kn.get(p["comp"], -1) >= p["ci"]:
                continue
            o["need"].append(d)
            p["sig"] = True
            for c, v in p["clock"].items():
                if kn.get(c, -1) < v:
                    kn[c] = v
            kn[p["comp"]] = max(kn.get(p["comp"], -1), p["ci"])
        o["clock"] = dict(kn)
    names = {"V": "sV", "A": "sA", "P": "sP", "G": "sG"}
    count = {}
    for o in ops:
        c = names.get(o["comp"], o["comp"])
        q = queues.get(o["q"])
        for d in o["need"]:
            p = ops[d]
            q.wait_ge(T.sem[names.get(p["comp"], p["comp"])], p["val"])
        if o["q"] == "N":
            count[c] = count.get(c, 0) + o["amt"]
            o["val"] = count[c]
            continue
        ins = o["fn"]()
        if o["comp"] == "sL":
            continue
        if o["sig"]:
            count[c] = count.get(c, 0) + o["amt"]
            o["val"] = count[c]
            ins.then_inc(T.sem[c], o["amt"])
    for c in count:
        g.wait_ge(T.sem[c], count[c])
    g.wait_ge(T.sem.sL, sent[0])
